import numpy as np
import ml_dtypes


def mxq(x, axis, fmt="e4m3"):
    dtype, down = {"e4m3": (ml_dtypes.float8_e4m3fn, 7), "e5m2": (ml_dtypes.float8_e5m2, 14)}[fmt]
    v = np.moveaxis(np.asarray(x, np.float32).astype(ml_dtypes.bfloat16).astype(np.float64), axis, -1)
    blocks = v.reshape(v.shape[:-1] + (-1, 32))
    amax = np.abs(blocks).max(-1, keepdims=True)
    byte = np.maximum(np.where(amax > 0, np.frexp(amax)[1] - 1 + 127, 0) - down, 1)
    scale = np.exp2(byte - 127.0)
    codes = (blocks / scale).astype(np.float32).astype(dtype).astype(np.float64)
    return np.moveaxis((codes * scale).reshape(v.shape), -1, axis)


WIDE = False


def mx_kscale(k):
    if not WIDE:
        return np.ones(k)
    levels = np.array([10, -10, 5, -5, 0])
    if k % 512:
        return np.exp2(np.random.permutation(np.resize(levels, k // 32))).repeat(32)
    a = np.empty((k // 512, 16))
    for p in range(k // 512):
        a[p, :8] = np.random.permutation(np.resize(levels, 8))
        for g in range(8):
            far = levels[np.abs(levels - a[p, g]) >= 10]
            a[p, g + 8] = far[np.random.randint(len(far))]
    return np.exp2(a.ravel()).repeat(32)


def f64(x):
    return np.asarray(x).astype(np.float64)


def striped(idx):
    return np.tile(idx.reshape(-1, 16).T, (8, 1)).astype(np.uint16)


def unstriped(offs):
    return offs[:16].T.reshape(-1).astype(np.int64)


E2M1 = np.array([0.0, 0.5, 1.0, 1.5, 2.0, 3.0, 4.0, 6.0, -0.0, -0.5, -1.0, -1.5, -2.0, -3.0, -4.0, -6.0])


def pack_weight(w, fmt):
    k, n = w.shape
    w = f64(np.asarray(w, np.float32).astype(ml_dtypes.bfloat16)).reshape(k // 32, 32, n)
    amax = np.abs(w).max(1)
    if fmt == "e4m3":
        byte = np.frexp(amax)[1] - 1 + 127 - 7
    else:
        mant, ex = np.frexp(amax / 6.0)
        byte = np.where(mant > 0.5, ex, ex - 1) + 127
    byte = np.clip(np.where(amax > 0, byte, 1), 1, 254)
    scaled = (w * np.exp2(127.0 - byte)[:, None, :]).reshape(k, n).astype(np.float32)
    by_word = np.ascontiguousarray(scaled.reshape(k // 512, 128, 4, n).transpose(0, 1, 3, 2))
    if fmt == "e4m3":
        words = by_word.astype(ml_dtypes.float8_e4m3fn).view(np.uint8)
    else:
        c = by_word.astype(ml_dtypes.float4_e2m1fn).view(np.uint8) & 0xF
        words = (c[..., 0::2] | (c[..., 1::2] << 4)).reshape(k // 512, 128, 2 * n)
    return np.ascontiguousarray(words), np.ascontiguousarray(byte.astype(np.uint8).reshape(k // 512, 16, n))


def unpack_weight(words, scales, fmt):
    g, _, n = scales.shape
    words = np.ascontiguousarray(words).reshape(g, 128, n, -1)
    if fmt == "e4m3":
        vals = words.view(ml_dtypes.float8_e4m3fn).astype(np.float64)
    else:
        nib = np.empty((g, 128, n, 4), np.uint8)
        nib[..., 0::2] = words & 0xF
        nib[..., 1::2] = words >> 4
        vals = E2M1[nib]
    vals = vals * np.repeat(np.exp2(scales.astype(np.float64) - 127.0), 8, axis=1)[..., None]
    return vals.transpose(0, 1, 3, 2).reshape(g * 512, n)


def relu(v):
    return np.maximum(v, 0.0)


K, T, E, C, H, N = 1536, 640, 10, 128, 512, 128


def by_expert(wq, xq):
    return np.concatenate([wq[e].T @ xq[:, e * C:(e + 1) * C] for e in range(E)], axis=1)


def setup_inputs():
    n = np.random.standard_normal
    s = mx_kscale(K)[:, None]
    u = mx_kscale(H)
    first = np.random.permutation(np.repeat(np.arange(E), T // E))
    second = (first + 1 + np.random.permutation(np.repeat(np.arange(E - 1), -(-T // (E - 1)))[:T])) % E
    while np.bincount(second, minlength=E).max() != T // E:
        load = np.bincount(second, minlength=E); hi, lo = int(load.argmax()), int(load.argmin())
        t = np.flatnonzero((second == hi) & (first != lo))[0]; second[t] = lo
    slot_token = np.empty(E * C, np.int64); pos = np.empty((2, T), np.int64); fill = np.zeros(E, np.int64)
    place = np.stack([np.random.permutation(C) for _ in range(E)])
    for r, deal in enumerate((first, second)):
        for t in np.random.permutation(T):
            e = deal[t]; j = e * C + place[e, fill[e]]; fill[e] += 1; slot_token[j] = t; pos[r, t] = j
    g = np.random.uniform(0.2, 0.8, T)
    x = pack_weight(n((K, T)) * s, "e4m3")
    return {
        "x_words": x[0],
        "x_scales": x[1],
        "w1": (n((E + 1, K, H)) / np.sqrt(K) / s[None] * u[None, None, :]).astype(np.float32),
        "w2": (n((E + 1, H, N)) / np.sqrt(H) / u[None, :, None]).astype(np.float32),
        "gate": np.stack([np.tile(g, (N, 1)), np.tile(1.0 - g, (N, 1))]).astype(np.float32),
        "offs": striped(slot_token),
        "pos1": striped(pos[0]),
        "pos2": striped(pos[1]),
    }


def reference(x_words, x_scales, w1, w2, gate, offs, pos1, pos2):
    idx = unstriped(offs)
    w1q, w2q = mxq(f64(w1), 1, "e4m3"), mxq(f64(w2), 1, "e4m3")
    xs = unpack_weight(x_words, x_scales, "e4m3")
    hs = relu(w1q[E].T @ xs)
    ys = w2q[E].T @ mxq(hs, 0, "e4m3")
    xq = unpack_weight(x_words, x_scales, "e4m3")[:, idx]
    h = relu(by_expert(w1q, xq))
    y = by_expert(w2q, mxq(h, 0, "e4m3"))
    return ys + f64(gate[0]) * y[:, unstriped(pos1)] + f64(gate[1]) * y[:, unstriped(pos2)]

@@ -1,0 +1,196 @@
+from contextlib import ExitStack
+
+import concourse.mybir as mybir
+
+K, T, E, C, H, N = 1536, 640, 10, 128, 512, 128
+FLOPS = 2 * (E * C + T) * (K * H + H * N)
+
+F32 = mybir.dt.float32
+BF16 = mybir.dt.bfloat16
+I32 = mybir.dt.int32
+U32 = mybir.dt.uint32
+U16 = mybir.dt.uint16
+U8 = mybir.dt.uint8
+FP8X4 = mybir.dt.float8_e4m3fn_x4
+MULT = mybir.AluOpType.mult
+ADD = mybir.AluOpType.add
+RELU = mybir.ActivationFunctionType.Relu
+
+P = 128
+PACK = 4
+PASSES = K // (P * PACK)
+SLOTS = E * C
+SHARED = E
+GATHER = 256
+SCALAR_M = 64
+WHOLE_LOADS = 8
+EARLY_W2 = 7
+LATE_W2 = ((0, 4), (4, 6), (6, 7))
+TOKEN_PARTS = ((0, 512), (512, 640))
+
+
+def tile_moe_shr_mlp_relu_kernel(tc, x_words, x_scales, w1, w2, gate, offs, pos1, pos2, out):
+    nc = tc.nc
+    with ExitStack() as ctx:
+        keep = ctx.enter_context(tc.tile_pool(name="keep", bufs=1))
+        stream = ctx.enter_context(tc.tile_pool(name="stream", bufs=4))
+        stage = ctx.enter_context(tc.tile_pool(name="stage", bufs=4))
+        codes = ctx.enter_context(tc.tile_pool(name="codes", bufs=7))
+        psum1 = ctx.enter_context(tc.psum_pool(name="psum1", bufs=4))
+        psum2 = ctx.enter_context(tc.psum_pool(name="psum2", bufs=2))
+        psum3 = ctx.enter_context(tc.psum_pool(name="psum3", bufs=1))
+
+        offs_sb = keep.tile([P, SLOTS // 16], U16, name="offs_sb")
+        pos1_sb = keep.tile([P, T // 16], U16, name="pos1_sb")
+        pos2_sb = keep.tile([P, T // 16], U16, name="pos2_sb")
+        tok_words = keep.tile([P, PASSES, T], I32, name="tok_words", align_bytes=64)
+        tok_scales = keep.tile([P, T], U8, name="tok_scales", align_bytes=64)
+        slot_words = keep.tile([P, PASSES, SLOTS], U32, name="slot_words", align_bytes=64)
+        slot_scales = keep.tile([P, SLOTS], U8, name="slot_scales", align_bytes=64)
+        h_codes = keep.tile([P, SLOTS + T], U32, name="h_codes", align_bytes=64)
+        h_scales = keep.tile([P, SLOTS + T], U8, name="h_scales", align_bytes=64)
+        w2_codes = keep.tile([P, E + 1, N], U32, name="w2_codes", align_bytes=64)
+        w2_scales = keep.tile([P, E + 1, N], U8, name="w2_scales", align_bytes=64)
+        w2_early = keep.tile([P, E - EARLY_W2, PACK * N], F32, name="w2_early", align_bytes=64)
+        y = keep.tile([P, SLOTS], F32, name="y", align_bytes=64)
+
+        w1_rows = w1.rearrange("e (o p j) c -> e p o (j c)", p=P, j=PACK)
+        w2_rows = w2.rearrange("e (p j) n -> p e (j n)", j=PACK)
+
+        scale_rows = keep.tile([P, T // 4], I32, name="scale_rows", align_bytes=64)
+
+        def load_token_scales():
+            nc.gpsimd.memset(tok_scales[:], 0)
+            scale_words = x_scales.bitcast(I32)
+            for q in range(4):
+                live = slice(32 * q, 32 * q + 4 * PASSES)
+                nc.sync.dma_start(out=scale_rows[live, :], in_=scale_words[:, 4 * q : 4 * q + 4, :])
+                nc.gpsimd.tensor_copy(out=tok_scales[live, :].bitcast(I32), in_=scale_rows[live, :])
+
+        nc.sync.dma_start(out=tok_words[:], in_=x_words.rearrange("o p t r -> p o (t r)").bitcast(I32))
+
+        def load_w1(e, whole):
+            raw = stream.tile([P, PASSES, PACK * H], F32, name="raw", tag="raw", align_bytes=64)
+            if whole:
+                nc.sync.dma_start(out=raw[:], in_=w1_rows[e])
+            else:
+                for o in range(PASSES):
+                    nc.sync.dma_start(out=raw[:, o, :], in_=w1_rows[e, :, o, :])
+                    if e == SHARED and o == 1:
+                        load_token_scales()
+                        nc.sync.dma_start(offs_sb[:], offs)
+            return raw
+
+        def round_w1(raw, o):
+            grouped = stage.tile([P, PACK * H], BF16, name="w1_bf16", align_bytes=64)
+            src = raw[:, o, :].rearrange("p (j m t) -> p m j t", j=PACK, t=PACK)
+            dst = grouped[:].rearrange("p (t m j) -> p m j t", j=PACK, t=PACK)
+            nc.scalar.copy(out=dst[:, :SCALAR_M], in_=src[:, :SCALAR_M])
+            nc.vector.tensor_copy(out=dst[:, SCALAR_M:], in_=src[:, SCALAR_M:])
+            return grouped
+
+        def quantize_w1(grouped):
+            w1_codes = codes.tile([P, H], U32, name="w1_codes", align_bytes=64)
+            w1_scales = codes.tile([P, H], U8, name="w1_scales", align_bytes=64)
+            nc.vector.quantize_mx(out=w1_codes[:].bitcast(FP8X4), scales=w1_scales[:], in_=grouped[:])
+            return w1_codes, w1_scales
+
+        def gather_slots(first):
+            cols = slice(first, first + GATHER)
+            listed = offs_sb[:, first // 16 : (first + GATHER) // 16]
+            for o in range(PASSES):
+                nc.vector.tensor_copy(slot_words[:, o, cols], tok_words[:, o, :].bitcast(U32).indirect(listed))
+            nc.vector.tensor_copy(slot_scales[:, cols], tok_scales[:].indirect(listed))
+
+        def first_layer(w1_q, words, scales, first, h_first):
+            acc = psum1.tile([P, PACK, C], F32, name="acc1")
+            cols = slice(first, first + C)
+            for t in range(PACK):
+                for o in range(PASSES):
+                    w1_codes, w1_scales = w1_q[o]
+                    nc.tensor.matmul_mx(
+                        out=acc[:, t, :],
+                        lhsT=w1_codes[:, t * P : (t + 1) * P].bitcast(FP8X4),
+                        lhsT_scale=w1_scales[:, t * P : (t + 1) * P],
+                        rhs=words[:, o, cols].bitcast(FP8X4),
+                        rhs_scale=scales[4 * o :, cols],
+                        start=(o == 0),
+                        stop=(o == PASSES - 1),
+                    )
+            h = stage.tile([P, C, PACK], BF16, name="h_bf16", align_bytes=64)
+            nc.scalar.activation(h[:], acc[:].rearrange("p t c -> p c t"), RELU)
+            h_cols = slice(h_first, h_first + C)
+            nc.vector.quantize_mx(out=h_codes[:, h_cols].bitcast(FP8X4), scales=h_scales[:, h_cols], in_=h[:].rearrange("p c t -> p (c t)"))
+
+        def quantize_w2(raw, e):
+            grouped = stage.tile([P, PACK * N], BF16, name="w2_bf16", align_bytes=64)
+            nc.scalar.copy(
+                out=grouped[:].rearrange("p (c i j) -> p c j i", i=4, j=PACK),
+                in_=raw.rearrange("p (j c i) -> p c j i", i=4, j=PACK),
+            )
+            nc.vector.quantize_mx(out=w2_codes[:, e, :].bitcast(FP8X4), scales=w2_scales[:, e, :], in_=grouped[:])
+
+        def second_layer(acc, e, h_cols):
+            nc.tensor.matmul_mx(
+                out=acc,
+                lhsT=w2_codes[:, e, :].bitcast(FP8X4),
+                lhsT_scale=w2_scales[:, e, :],
+                rhs=h_codes[:, h_cols].bitcast(FP8X4),
+                rhs_scale=h_scales[:, h_cols],
+                start=True,
+                stop=True,
+            )
+
+        def routed_results(e0, e1):
+            acc = psum2.tile([P, (e1 - e0) * C], F32, name="acc2")
+            for e in range(e0, e1):
+                second_layer(acc[:, (e - e0) * C : (e - e0 + 1) * C], e, slice(e * C, (e + 1) * C))
+            nc.scalar.copy(out=y[:, e0 * C : e1 * C], in_=acc[:])
+
+        for step, e in enumerate([SHARED] + list(range(E))):
+            raw = load_w1(e, 0 < step < WHOLE_LOADS)
+            if step == 1:
+                nc.sync.dma_start(pos1_sb[:], pos1)
+                nc.sync.dma_start(pos2_sb[:], pos2)
+                nc.sync.dma_start(out=w2_early[:], in_=w2_rows[:, EARLY_W2:E, :])
+            if e != SHARED and (e * C) % GATHER == 0:
+                gather_slots(e * C)
+            w1_q = [quantize_w1(round_w1(raw, o)) for o in range(PASSES)]
+            if e == SHARED:
+                for first in range(0, T, C):
+                    first_layer(w1_q, tok_words, tok_scales, first, SLOTS + first)
+            else:
+                first_layer(w1_q, slot_words, slot_scales, e * C, e * C)
+            if step == 1:
+                for late in range(EARLY_W2, E):
+                    quantize_w2(w2_early[:, late - EARLY_W2, :], late)
+            if EARLY_W2 <= e < E:
+                routed_results(e, e + 1)
+
+        gate_first = (EARLY_W2 + 1) * PACK * N
+        last = stream.tile([P, gate_first + 2 * T], F32, name="last", tag="raw", align_bytes=64)
+        w2_late = last[:, :gate_first].rearrange("p (e w) -> p e w", w=PACK * N)
+        gates = last[:, gate_first:].rearrange("p (r t) -> p r t", t=T)
+        for e0, e1 in LATE_W2:
+            nc.sync.dma_start(out=w2_late[:, e0:e1, :], in_=w2_rows[:, e0:e1, :])
+        nc.sync.dma_start(out=gates, in_=gate.rearrange("r p t -> p r t"))
+        nc.sync.dma_start(out=w2_late[:, EARLY_W2, :], in_=w2_rows[:, SHARED, :])
+        for e0, e1 in LATE_W2:
+            for e in range(e0, e1):
+                quantize_w2(w2_late[:, e, :], e)
+            routed_results(e0, e1)
+        quantize_w2(w2_late[:, EARLY_W2, :], SHARED)
+
+        for part, (t0, t1) in enumerate(TOKEN_PARTS):
+            width = t1 - t0
+            ys = psum3.tile([P, width], F32, name="ys%d" % part)
+            second_layer(ys[:], SHARED, slice(SLOTS + t0, SLOTS + t1))
+            first_term = keep.tile([P, width], F32, name="first_term%d" % part)
+            second_term = keep.tile([P, width], F32, name="second_term%d" % part)
+            partial = keep.tile([P, width], F32, name="partial%d" % part)
+            result = keep.tile([P, width], F32, name="result%d" % part)
+            nc.vector.tensor_tensor(first_term[:], y[:].indirect(pos1_sb[:, t0 // 16 : t1 // 16]), gates[:, 0, t0:t1], MULT)
+            nc.vector.tensor_tensor(second_term[:], y[:].indirect(pos2_sb[:, t0 // 16 : t1 // 16]), gates[:, 1, t0:t1], MULT)
+            nc.vector.tensor_tensor(partial[:], ys[:], first_term[:], ADD)
+            nc.vector.tensor_tensor(result[:], partial[:], second_term[:], ADD)
+            nc.sync.dma_start(out=out[:, t0:t1], in_=result[:])

@@ -22,10 +22,9 @@ PASSES = K // (P * PACK)
 SLOTS = E * C
 SHARED = E
 GATHER = 256
-SCALAR_M = 64
 WHOLE_LOADS = 8
-EARLY_W2 = 7
-LATE_W2 = ((0, 4), (4, 6), (6, 7))
+EARLY_W2 = 6
+LATE_W2 = ((0, 2), (2, 4), (4, 5), (5, 6))
 TOKEN_PARTS = ((0, 512), (512, 640))
 
 
@@ -34,7 +33,8 @@ def tile_moe_shr_mlp_relu_kernel(tc, x_words, x_scales, w1, w2, gate, offs, pos1
     with ExitStack() as ctx:
         keep = ctx.enter_context(tc.tile_pool(name="keep", bufs=1))
         stream = ctx.enter_context(tc.tile_pool(name="stream", bufs=4))
-        stage = ctx.enter_context(tc.tile_pool(name="stage", bufs=4))
+        stage = ctx.enter_context(tc.tile_pool(name="stage", bufs=5))
+        gathered = ctx.enter_context(tc.tile_pool(name="gathered", bufs=3))
         codes = ctx.enter_context(tc.tile_pool(name="codes", bufs=7))
         psum1 = ctx.enter_context(tc.psum_pool(name="psum1", bufs=4))
         psum2 = ctx.enter_context(tc.psum_pool(name="psum2", bufs=2))
@@ -45,12 +45,10 @@ def tile_moe_shr_mlp_relu_kernel(tc, x_words, x_scales, w1, w2, gate, offs, pos1
         pos2_sb = keep.tile([P, T // 16], U16, name="pos2_sb")
         tok_words = keep.tile([P, PASSES, T], I32, name="tok_words", align_bytes=64)
         tok_scales = keep.tile([P, T], U8, name="tok_scales", align_bytes=64)
-        slot_words = keep.tile([P, PASSES, SLOTS], U32, name="slot_words", align_bytes=64)
-        slot_scales = keep.tile([P, SLOTS], U8, name="slot_scales", align_bytes=64)
         h_codes = keep.tile([P, SLOTS + T], U32, name="h_codes", align_bytes=64)
         h_scales = keep.tile([P, SLOTS + T], U8, name="h_scales", align_bytes=64)
-        w2_codes = keep.tile([P, E + 1, N], U32, name="w2_codes", align_bytes=64)
-        w2_scales = keep.tile([P, E + 1, N], U8, name="w2_scales", align_bytes=64)
+        w2_codes = keep.tile([P, (E + 1) * N], U32, name="w2_codes", align_bytes=64)
+        w2_scales = keep.tile([P, (E + 1) * N], U8, name="w2_scales", align_bytes=64)
         w2_early = keep.tile([P, E - EARLY_W2, PACK * N], F32, name="w2_early", align_bytes=64)
         y = keep.tile([P, SLOTS], F32, name="y", align_bytes=64)
 
@@ -68,6 +66,7 @@ def tile_moe_shr_mlp_relu_kernel(tc, x_words, x_scales, w1, w2, gate, offs, pos1
                 nc.gpsimd.tensor_copy(out=tok_scales[live, :].bitcast(I32), in_=scale_rows[live, :])
 
         nc.sync.dma_start(out=tok_words[:], in_=x_words.rearrange("o p t r -> p o (t r)").bitcast(I32))
+        nc.sync.dma_start(offs_sb[:], offs)
 
         def load_w1(e, whole):
             raw = stream.tile([P, PASSES, PACK * H], F32, name="raw", tag="raw", align_bytes=64)
@@ -76,37 +75,41 @@ def tile_moe_shr_mlp_relu_kernel(tc, x_words, x_scales, w1, w2, gate, offs, pos1
             else:
                 for o in range(PASSES):
                     nc.sync.dma_start(out=raw[:, o, :], in_=w1_rows[e, :, o, :])
-                    if e == SHARED and o == 1:
+                    if e == SHARED and o == 0:
                         load_token_scales()
-                        nc.sync.dma_start(offs_sb[:], offs)
             return raw
 
         def round_w1(raw, o):
             grouped = stage.tile([P, PACK * H], BF16, name="w1_bf16", align_bytes=64)
             src = raw[:, o, :].rearrange("p (j m t) -> p m j t", j=PACK, t=PACK)
             dst = grouped[:].rearrange("p (t m j) -> p m j t", j=PACK, t=PACK)
-            nc.scalar.copy(out=dst[:, :SCALAR_M], in_=src[:, :SCALAR_M])
-            nc.vector.tensor_copy(out=dst[:, SCALAR_M:], in_=src[:, SCALAR_M:])
+            nc.scalar.copy(out=dst[:, :, :, :2], in_=src[:, :, :, :2])
+            nc.vector.tensor_copy(out=dst[:, :, :, 2:], in_=src[:, :, :, 2:])
             return grouped
 
-        def quantize_w1(grouped):
+        def quantize_w1(grouped, calls):
             w1_codes = codes.tile([P, H], U32, name="w1_codes", align_bytes=64)
             w1_scales = codes.tile([P, H], U8, name="w1_scales", align_bytes=64)
-            nc.vector.quantize_mx(out=w1_codes[:].bitcast(FP8X4), scales=w1_scales[:], in_=grouped[:])
+            width = H // calls
+            for first in range(H - width, -1, -width):
+                cols = slice(first, first + width)
+                nc.vector.quantize_mx(out=w1_codes[:, cols].bitcast(FP8X4), scales=w1_scales[:, cols], in_=grouped[:, PACK * first : PACK * (first + width)])
             return w1_codes, w1_scales
 
         def gather_slots(first):
-            cols = slice(first, first + GATHER)
+            slot_words = gathered.tile([P, PASSES, GATHER], U32, name="slot_words", align_bytes=64)
+            slot_scales = gathered.tile([P, GATHER], U8, name="slot_scales", align_bytes=64)
             listed = offs_sb[:, first // 16 : (first + GATHER) // 16]
             for o in range(PASSES):
-                nc.vector.tensor_copy(slot_words[:, o, cols], tok_words[:, o, :].bitcast(U32).indirect(listed))
-            nc.vector.tensor_copy(slot_scales[:, cols], tok_scales[:].indirect(listed))
+                nc.vector.tensor_copy(slot_words[:, o, :], tok_words[:, o, :].bitcast(U32).indirect(listed))
+            nc.vector.tensor_copy(slot_scales[:], tok_scales[:].indirect(listed))
+            return slot_words, slot_scales
 
-        def first_layer(w1_q, words, scales, first, h_first):
+        def first_layer(w1_q, words, scales, first):
             acc = psum1.tile([P, PACK, C], F32, name="acc1")
             cols = slice(first, first + C)
-            for t in range(PACK):
-                for o in range(PASSES):
+            for o in range(PASSES):
+                for t in reversed(range(PACK)):
                     w1_codes, w1_scales = w1_q[o]
                     nc.tensor.matmul_mx(
                         out=acc[:, t, :],
@@ -114,27 +117,44 @@ def tile_moe_shr_mlp_relu_kernel(tc, x_words, x_scales, w1, w2, gate, offs, pos1
                         lhsT_scale=w1_scales[:, t * P : (t + 1) * P],
                         rhs=words[:, o, cols].bitcast(FP8X4),
                         rhs_scale=scales[4 * o :, cols],
-                        start=(o == 0),
-                        stop=(o == PASSES - 1),
+                        start=(o == 0 and t == PACK - 1),
+                        stop=(o == PASSES - 1 and t == 0),
                     )
-            h = stage.tile([P, C, PACK], BF16, name="h_bf16", align_bytes=64)
-            nc.scalar.activation(h[:], acc[:].rearrange("p t c -> p c t"), RELU)
-            h_cols = slice(h_first, h_first + C)
-            nc.vector.quantize_mx(out=h_codes[:, h_cols].bitcast(FP8X4), scales=h_scales[:, h_cols], in_=h[:].rearrange("p c t -> p (c t)"))
+            return acc
 
-        def quantize_w2(raw, e):
-            grouped = stage.tile([P, PACK * N], BF16, name="w2_bf16", align_bytes=64)
-            nc.scalar.copy(
-                out=grouped[:].rearrange("p (c i j) -> p c j i", i=4, j=PACK),
-                in_=raw.rearrange("p (j c i) -> p c j i", i=4, j=PACK),
+        def hidden(acc, h, h_first):
+            nc.scalar.activation(h.rearrange("p (c t) -> p c t", t=PACK), acc[:].rearrange("p t c -> p c t"), RELU)
+            h_cols = slice(h_first, h_first + C)
+            nc.vector.quantize_mx(out=h_codes[:, h_cols].bitcast(FP8X4), scales=h_scales[:, h_cols], in_=h)
+
+        def fresh_h():
+            h = stage.tile([P, PACK * C], BF16, name="h_bf16", align_bytes=64)
+            return h[:]
+
+        def finish_routed(acc, h, e):
+            hidden(acc, h, e * C)
+            if e >= EARLY_W2:
+                routed_results(e, e + 1)
+
+        def quantize_w2(raw, e0, e1, on_scalar):
+            grouped = stage.tile([P, e1 - e0, PACK * N], BF16, name="w2_bf16", align_bytes=64)
+            for i in range(e1 - e0):
+                copy = nc.scalar.copy if i < on_scalar else nc.vector.tensor_copy
+                copy(
+                    out=grouped[:, i, :].rearrange("p (c i j) -> p c j i", i=4, j=PACK),
+                    in_=raw[:, i, :].rearrange("p (j c i) -> p c j i", i=4, j=PACK),
+                )
+            nc.vector.quantize_mx(
+                out=w2_codes[:, e0 * N : e1 * N].bitcast(FP8X4),
+                scales=w2_scales[:, e0 * N : e1 * N],
+                in_=grouped[:].rearrange("p e w -> p (e w)"),
             )
-            nc.vector.quantize_mx(out=w2_codes[:, e, :].bitcast(FP8X4), scales=w2_scales[:, e, :], in_=grouped[:])
 
         def second_layer(acc, e, h_cols):
             nc.tensor.matmul_mx(
                 out=acc,
-                lhsT=w2_codes[:, e, :].bitcast(FP8X4),
-                lhsT_scale=w2_scales[:, e, :],
+                lhsT=w2_codes[:, e * N : (e + 1) * N].bitcast(FP8X4),
+                lhsT_scale=w2_scales[:, e * N : (e + 1) * N],
                 rhs=h_codes[:, h_cols].bitcast(FP8X4),
                 rhs_scale=h_scales[:, h_cols],
                 start=True,
@@ -154,18 +174,21 @@ def tile_moe_shr_mlp_relu_kernel(tc, x_words, x_scales, w1, w2, gate, offs, pos1
                 nc.sync.dma_start(pos2_sb[:], pos2)
                 nc.sync.dma_start(out=w2_early[:], in_=w2_rows[:, EARLY_W2:E, :])
             if e != SHARED and (e * C) % GATHER == 0:
-                gather_slots(e * C)
-            w1_q = [quantize_w1(round_w1(raw, o)) for o in range(PASSES)]
+                slot_words, slot_scales = gather_slots(e * C)
+            w1_q = []
+            for o in range(PASSES):
+                grouped = round_w1(raw, o)
+                w1_q.append(quantize_w1(grouped, 2 if (e, o) == (E - 1, PASSES - 1) else 1))
+                if o == 0 and step >= 2:
+                    finish_routed(acc, grouped[:, : PACK * C], e - 1)
             if e == SHARED:
                 for first in range(0, T, C):
-                    first_layer(w1_q, tok_words, tok_scales, first, SLOTS + first)
+                    hidden(first_layer(w1_q, tok_words, tok_scales, first), fresh_h(), SLOTS + first)
             else:
-                first_layer(w1_q, slot_words, slot_scales, e * C, e * C)
+                acc = first_layer(w1_q, slot_words, slot_scales, (e * C) % GATHER)
             if step == 1:
-                for late in range(EARLY_W2, E):
-                    quantize_w2(w2_early[:, late - EARLY_W2, :], late)
-            if EARLY_W2 <= e < E:
-                routed_results(e, e + 1)
+                quantize_w2(w2_early[:], EARLY_W2, E, E - EARLY_W2)
+        finish_routed(acc, fresh_h(), E - 1)
 
         gate_first = (EARLY_W2 + 1) * PACK * N
         last = stream.tile([P, gate_first + 2 * T], F32, name="last", tag="raw", align_bytes=64)
@@ -173,13 +196,13 @@ def tile_moe_shr_mlp_relu_kernel(tc, x_words, x_scales, w1, w2, gate, offs, pos1
         gates = last[:, gate_first:].rearrange("p (r t) -> p r t", t=T)
         for e0, e1 in LATE_W2:
             nc.sync.dma_start(out=w2_late[:, e0:e1, :], in_=w2_rows[:, e0:e1, :])
-        nc.sync.dma_start(out=gates, in_=gate.rearrange("r p t -> p r t"))
         nc.sync.dma_start(out=w2_late[:, EARLY_W2, :], in_=w2_rows[:, SHARED, :])
+        for r in range(2):
+            nc.sync.dma_start(out=gates[:, r, :], in_=gate[r])
         for e0, e1 in LATE_W2:
-            for e in range(e0, e1):
-                quantize_w2(w2_late[:, e, :], e)
+            quantize_w2(w2_late[:, e0:e1, :], e0, e1, (e1 - e0) // 2)
             routed_results(e0, e1)
-        quantize_w2(w2_late[:, EARLY_W2, :], SHARED)
+        quantize_w2(w2_late[:, EARLY_W2:, :], SHARED, SHARED + 1, 1)
 
         for part, (t0, t1) in enumerate(TOKEN_PARTS):
             width = t1 - t0
@@ -191,6 +214,6 @@ def tile_moe_shr_mlp_relu_kernel(tc, x_words, x_scales, w1, w2, gate, offs, pos1
             result = keep.tile([P, width], F32, name="result%d" % part)
             nc.vector.tensor_tensor(first_term[:], y[:].indirect(pos1_sb[:, t0 // 16 : t1 // 16]), gates[:, 0, t0:t1], MULT)
             nc.vector.tensor_tensor(second_term[:], y[:].indirect(pos2_sb[:, t0 // 16 : t1 // 16]), gates[:, 1, t0:t1], MULT)
-            nc.vector.tensor_tensor(partial[:], ys[:], first_term[:], ADD)
-            nc.vector.tensor_tensor(result[:], partial[:], second_term[:], ADD)
+            nc.vector.tensor_tensor(partial[:], first_term[:], second_term[:], ADD)
+            nc.vector.tensor_tensor(result[:], ys[:], partial[:], ADD)
             nc.sync.dma_start(out=out[:, t0:t1], in_=result[:])

@@ -23,8 +23,11 @@ SLOTS = E * C
 SHARED = E
 GATHER = 256
 WHOLE_LOADS = 8
-EARLY_W2 = 6
-LATE_W2 = ((0, 2), (2, 4), (4, 5), (5, 6))
+UNDELAYED = (5, 6, 7,)
+HALVED = ((8, 1), (9, 1), (9, 2),)
+W2_LOADS = ((0, 2), (2, 3), (3, 4), (4, 6), (6, 8), (8, 9), (9, 10), (10, 11))
+W2_ON_SCALAR = (0, 3, 5, 6, 9, 10,)
+TAIL = (("q", 0, 2, False), ("q", 2, 3, False), ("q", 3, 4, False), ("y", 0, 4, False), ("q", 4, 5, False), ("q", 5, 7, False), ("y", 4, 7, False), ("q", 7, 9, False), ("y", 7, 8, True), ("q", 9, 10, False), ("y", 8, 10, False), ("q", 10, 11, False))
 TOKEN_PARTS = ((0, 512), (512, 640))
 
 
@@ -33,12 +36,10 @@ def tile_moe_shr_mlp_relu_kernel(tc, x_words, x_scales, w1, w2, gate, offs, pos1
     with ExitStack() as ctx:
         keep = ctx.enter_context(tc.tile_pool(name="keep", bufs=1))
         stream = ctx.enter_context(tc.tile_pool(name="stream", bufs=4))
-        stage = ctx.enter_context(tc.tile_pool(name="stage", bufs=5))
-        gathered = ctx.enter_context(tc.tile_pool(name="gathered", bufs=3))
+        stage = ctx.enter_context(tc.tile_pool(name="stage", bufs=6))
+        gathered = ctx.enter_context(tc.tile_pool(name="gathered", bufs=5))
         codes = ctx.enter_context(tc.tile_pool(name="codes", bufs=7))
-        psum1 = ctx.enter_context(tc.psum_pool(name="psum1", bufs=4))
-        psum2 = ctx.enter_context(tc.psum_pool(name="psum2", bufs=2))
-        psum3 = ctx.enter_context(tc.psum_pool(name="psum3", bufs=1))
+        psum = ctx.enter_context(tc.psum_pool(name="psum", bufs=8))
 
         offs_sb = keep.tile([P, SLOTS // 16], U16, name="offs_sb")
         pos1_sb = keep.tile([P, T // 16], U16, name="pos1_sb")
@@ -49,7 +50,6 @@ def tile_moe_shr_mlp_relu_kernel(tc, x_words, x_scales, w1, w2, gate, offs, pos1
         h_scales = keep.tile([P, SLOTS + T], U8, name="h_scales", align_bytes=64)
         w2_codes = keep.tile([P, (E + 1) * N], U32, name="w2_codes", align_bytes=64)
         w2_scales = keep.tile([P, (E + 1) * N], U8, name="w2_scales", align_bytes=64)
-        w2_early = keep.tile([P, E - EARLY_W2, PACK * N], F32, name="w2_early", align_bytes=64)
         y = keep.tile([P, SLOTS], F32, name="y", align_bytes=64)
 
         w1_rows = w1.rearrange("e (o p j) c -> e p o (j c)", p=P, j=PACK)
@@ -87,9 +87,9 @@ def tile_moe_shr_mlp_relu_kernel(tc, x_words, x_scales, w1, w2, gate, offs, pos1
             nc.vector.tensor_copy(out=dst[:, :, :, 2:], in_=src[:, :, :, 2:])
             return grouped
 
-        def quantize_w1(grouped, calls):
-            w1_codes = codes.tile([P, H], U32, name="w1_codes", align_bytes=64)
-            w1_scales = codes.tile([P, H], U8, name="w1_scales", align_bytes=64)
+        def quantize_w1(grouped, calls, pool, name):
+            w1_codes = pool.tile([P, H], U32, name=name + "_codes", align_bytes=64)
+            w1_scales = pool.tile([P, H], U8, name=name + "_scales", align_bytes=64)
             width = H // calls
             for first in range(H - width, -1, -width):
                 cols = slice(first, first + width)
@@ -106,7 +106,7 @@ def tile_moe_shr_mlp_relu_kernel(tc, x_words, x_scales, w1, w2, gate, offs, pos1
             return slot_words, slot_scales
 
         def first_layer(w1_q, words, scales, first):
-            acc = psum1.tile([P, PACK, C], F32, name="acc1")
+            acc = psum.tile([P, PACK, C], F32, name="acc1", tag="bank")
             cols = slice(first, first + C)
             for o in range(PASSES):
                 for t in reversed(range(PACK)):
@@ -122,8 +122,11 @@ def tile_moe_shr_mlp_relu_kernel(tc, x_words, x_scales, w1, w2, gate, offs, pos1
                     )
             return acc
 
-        def hidden(acc, h, h_first):
-            nc.scalar.activation(h.rearrange("p (c t) -> p c t", t=PACK), acc[:].rearrange("p t c -> p c t"), RELU)
+        def hidden(acc, h, h_first, on_vector=False):
+            if on_vector:
+                nc.vector.tensor_scalar_max(h.rearrange("p (c t) -> p c t", t=PACK), acc[:].rearrange("p t c -> p c t"), 0.0)
+            else:
+                nc.scalar.activation(h.rearrange("p (c t) -> p c t", t=PACK), acc[:].rearrange("p t c -> p c t"), RELU)
             h_cols = slice(h_first, h_first + C)
             nc.vector.quantize_mx(out=h_codes[:, h_cols].bitcast(FP8X4), scales=h_scales[:, h_cols], in_=h)
 
@@ -131,18 +134,13 @@ def tile_moe_shr_mlp_relu_kernel(tc, x_words, x_scales, w1, w2, gate, offs, pos1
             h = stage.tile([P, PACK * C], BF16, name="h_bf16", align_bytes=64)
             return h[:]
 
-        def finish_routed(acc, h, e):
-            hidden(acc, h, e * C)
-            if e >= EARLY_W2:
-                routed_results(e, e + 1)
-
-        def quantize_w2(raw, e0, e1, on_scalar):
+        def quantize_w2(raw, e0, e1):
             grouped = stage.tile([P, e1 - e0, PACK * N], BF16, name="w2_bf16", align_bytes=64)
             for i in range(e1 - e0):
-                copy = nc.scalar.copy if i < on_scalar else nc.vector.tensor_copy
+                copy = nc.scalar.copy if e0 + i in W2_ON_SCALAR else nc.vector.tensor_copy
                 copy(
                     out=grouped[:, i, :].rearrange("p (c i j) -> p c j i", i=4, j=PACK),
-                    in_=raw[:, i, :].rearrange("p (j c i) -> p c j i", i=4, j=PACK),
+                    in_=raw[:, e0 + i, :].rearrange("p (j c i) -> p c j i", i=4, j=PACK),
                 )
             nc.vector.quantize_mx(
                 out=w2_codes[:, e0 * N : e1 * N].bitcast(FP8X4),
@@ -161,52 +159,57 @@ def tile_moe_shr_mlp_relu_kernel(tc, x_words, x_scales, w1, w2, gate, offs, pos1
                 stop=True,
             )
 
-        def routed_results(e0, e1):
-            acc = psum2.tile([P, (e1 - e0) * C], F32, name="acc2")
+        def routed_results(e0, e1, copy):
+            acc = psum.tile([P, (e1 - e0) * C], F32, name="acc2", tag="bank")
             for e in range(e0, e1):
                 second_layer(acc[:, (e - e0) * C : (e - e0 + 1) * C], e, slice(e * C, (e + 1) * C))
-            nc.scalar.copy(out=y[:, e0 * C : e1 * C], in_=acc[:])
+            copy(out=y[:, e0 * C : e1 * C], in_=acc[:])
 
         for step, e in enumerate([SHARED] + list(range(E))):
             raw = load_w1(e, 0 < step < WHOLE_LOADS)
             if step == 1:
                 nc.sync.dma_start(pos1_sb[:], pos1)
                 nc.sync.dma_start(pos2_sb[:], pos2)
-                nc.sync.dma_start(out=w2_early[:], in_=w2_rows[:, EARLY_W2:E, :])
             if e != SHARED and (e * C) % GATHER == 0:
                 slot_words, slot_scales = gather_slots(e * C)
             w1_q = []
             for o in range(PASSES):
                 grouped = round_w1(raw, o)
-                w1_q.append(quantize_w1(grouped, 2 if (e, o) == (E - 1, PASSES - 1) else 1))
-                if o == 0 and step >= 2:
-                    finish_routed(acc, grouped[:, : PACK * C], e - 1)
+                if e == SHARED:
+                    w1_q.append(quantize_w1(grouped, 1, keep, "shared%d" % o))
+                else:
+                    w1_q.append(quantize_w1(grouped, 2 if (e, o) in HALVED else 1, codes, "w1"))
+                if o == 1 and 1 <= step <= T // C:
+                    hidden(shared_acc, grouped[:, PACK * C : 2 * PACK * C], SLOTS + (step - 1) * C)
+                if o == 0 and step >= 2 and e - 1 in UNDELAYED:
+                    hidden(acc, fresh_h(), (e - 1) * C)
+                if o == 1 and step >= 2 and e - 1 not in UNDELAYED:
+                    hidden(acc, grouped[:, : PACK * C], (e - 1) * C)
             if e == SHARED:
-                for first in range(0, T, C):
-                    hidden(first_layer(w1_q, tok_words, tok_scales, first), fresh_h(), SLOTS + first)
-            else:
+                shared_q = w1_q
+            if step < T // C:
+                shared_acc = first_layer(shared_q, tok_words, tok_scales, step * C)
+            if e != SHARED:
                 acc = first_layer(w1_q, slot_words, slot_scales, (e * C) % GATHER)
-            if step == 1:
-                quantize_w2(w2_early[:], EARLY_W2, E, E - EARLY_W2)
-        finish_routed(acc, fresh_h(), E - 1)
+        hidden(acc, fresh_h(), (E - 1) * C)
 
-        gate_first = (EARLY_W2 + 1) * PACK * N
+        gate_first = (E + 1) * PACK * N
         last = stream.tile([P, gate_first + 2 * T], F32, name="last", tag="raw", align_bytes=64)
-        w2_late = last[:, :gate_first].rearrange("p (e w) -> p e w", w=PACK * N)
+        w2_raw = last[:, :gate_first].rearrange("p (e w) -> p e w", w=PACK * N)
         gates = last[:, gate_first:].rearrange("p (r t) -> p r t", t=T)
-        for e0, e1 in LATE_W2:
-            nc.sync.dma_start(out=w2_late[:, e0:e1, :], in_=w2_rows[:, e0:e1, :])
-        nc.sync.dma_start(out=w2_late[:, EARLY_W2, :], in_=w2_rows[:, SHARED, :])
+        for e0, e1 in W2_LOADS:
+            nc.sync.dma_start(out=w2_raw[:, e0:e1, :], in_=w2_rows[:, e0:e1, :])
         for r in range(2):
             nc.sync.dma_start(out=gates[:, r, :], in_=gate[r])
-        for e0, e1 in LATE_W2:
-            quantize_w2(w2_late[:, e0:e1, :], e0, e1, (e1 - e0) // 2)
-            routed_results(e0, e1)
-        quantize_w2(w2_late[:, EARLY_W2:, :], SHARED, SHARED + 1, 1)
+        for kind, e0, e1, on_vector in TAIL:
+            if kind == "q":
+                quantize_w2(w2_raw, e0, e1)
+            else:
+                routed_results(e0, e1, nc.vector.tensor_copy if on_vector else nc.scalar.copy)
 
         for part, (t0, t1) in enumerate(TOKEN_PARTS):
             width = t1 - t0
-            ys = psum3.tile([P, width], F32, name="ys%d" % part)
+            ys = psum.tile([P, width], F32, name="ys", tag="bank")
             second_layer(ys[:], SHARED, slice(SLOTS + t0, SLOTS + t1))
             first_term = keep.tile([P, width], F32, name="first_term%d" % part)
             second_term = keep.tile([P, width], F32, name="second_term%d" % part)

@@ -22,12 +22,13 @@ PASSES = K // (P * PACK)
 SLOTS = E * C
 SHARED = E
 GATHER = 256
-WHOLE_LOADS = 8
-UNDELAYED = (5, 6, 7,)
-HALVED = ((8, 1), (9, 1), (9, 2),)
-W2_LOADS = ((0, 2), (2, 3), (3, 4), (4, 6), (6, 8), (8, 9), (9, 10), (10, 11))
-W2_ON_SCALAR = (0, 3, 5, 6, 9, 10,)
-TAIL = (("q", 0, 2, False), ("q", 2, 3, False), ("q", 3, 4, False), ("y", 0, 4, False), ("q", 4, 5, False), ("q", 5, 7, False), ("y", 4, 7, False), ("q", 7, 9, False), ("y", 7, 8, True), ("q", 9, 10, False), ("y", 8, 10, False), ("q", 10, 11, False))
+WHOLE_LOADS = 9
+RELU_AFTER_PASS = (1, 1, 1, 1, 1, 0, 1, 0, 0)
+LAST_RELU_AFTER = 2
+HALVED = ((9, 0), (9, 1), (9, 2),)
+W2_LOADS = ((0, 2), (2, 3), (3, 4), (4, 6), (6, 7), (7, 8), (8, 10), (10, 11))
+W2_ON_SCALAR = (0, 2, 3, 4, 6, 7, 9, 10,)
+TAIL = (("q", 0, 2, False), ("q", 2, 3, False), ("q", 3, 5, False), ("y", 0, 4, False), ("q", 5, 6, False), ("q", 6, 7, False), ("q", 7, 8, False), ("y", 4, 8, False), ("q", 8, 9, False), ("y", 8, 9, True), ("q", 9, 10, False), ("y", 9, 10, True), ("q", 10, 11, False))
 TOKEN_PARTS = ((0, 512), (512, 640))
 
 
@@ -75,8 +76,6 @@ def tile_moe_shr_mlp_relu_kernel(tc, x_words, x_scales, w1, w2, gate, offs, pos1
             else:
                 for o in range(PASSES):
                     nc.sync.dma_start(out=raw[:, o, :], in_=w1_rows[e, :, o, :])
-                    if e == SHARED and o == 0:
-                        load_token_scales()
             return raw
 
         def round_w1(raw, o):
@@ -130,23 +129,27 @@ def tile_moe_shr_mlp_relu_kernel(tc, x_words, x_scales, w1, w2, gate, offs, pos1
             h_cols = slice(h_first, h_first + C)
             nc.vector.quantize_mx(out=h_codes[:, h_cols].bitcast(FP8X4), scales=h_scales[:, h_cols], in_=h)
 
-        def fresh_h():
-            h = stage.tile([P, PACK * C], BF16, name="h_bf16", align_bytes=64)
-            return h[:]
-
         def quantize_w2(raw, e0, e1):
-            grouped = stage.tile([P, e1 - e0, PACK * N], BF16, name="w2_bf16", align_bytes=64)
-            for i in range(e1 - e0):
-                copy = nc.scalar.copy if e0 + i in W2_ON_SCALAR else nc.vector.tensor_copy
-                copy(
-                    out=grouped[:, i, :].rearrange("p (c i j) -> p c j i", i=4, j=PACK),
-                    in_=raw[:, e0 + i, :].rearrange("p (j c i) -> p c j i", i=4, j=PACK),
+            grouped = stage.tile([P, e1 - e0, PACK * N], BF16, name="w2_bf16", bufs=6, align_bytes=64)
+            on_vector = [e for e in range(e0, e1) if e not in W2_ON_SCALAR]
+            for e in range(e0, e1):
+                if e in W2_ON_SCALAR:
+                    nc.scalar.copy(
+                        out=grouped[:, e - e0, :].rearrange("p (c i j) -> p c j i", i=4, j=PACK),
+                        in_=raw[:, e, :].rearrange("p (j c i) -> p c j i", i=4, j=PACK),
+                    )
+            if on_vector:
+                v0, v1 = on_vector[0], on_vector[-1] + 1
+                nc.vector.tensor_copy(
+                    out=grouped[:, v0 - e0 : v1 - e0, :].rearrange("p e (n j) -> p e n j", j=PACK),
+                    in_=raw[:, v0:v1, :].rearrange("p e (j n) -> p e n j", j=PACK),
                 )
             nc.vector.quantize_mx(
                 out=w2_codes[:, e0 * N : e1 * N].bitcast(FP8X4),
                 scales=w2_scales[:, e0 * N : e1 * N],
                 in_=grouped[:].rearrange("p e w -> p (e w)"),
             )
+            return grouped
 
         def second_layer(acc, e, h_cols):
             nc.tensor.matmul_mx(
@@ -166,7 +169,9 @@ def tile_moe_shr_mlp_relu_kernel(tc, x_words, x_scales, w1, w2, gate, offs, pos1
             copy(out=y[:, e0 * C : e1 * C], in_=acc[:])
 
         for step, e in enumerate([SHARED] + list(range(E))):
-            raw = load_w1(e, 0 < step < WHOLE_LOADS)
+            raw = load_w1(e, step < WHOLE_LOADS)
+            if step == 0:
+                load_token_scales()
             if step == 1:
                 nc.sync.dma_start(pos1_sb[:], pos1)
                 nc.sync.dma_start(pos2_sb[:], pos2)
@@ -181,9 +186,7 @@ def tile_moe_shr_mlp_relu_kernel(tc, x_words, x_scales, w1, w2, gate, offs, pos1
                     w1_q.append(quantize_w1(grouped, 2 if (e, o) in HALVED else 1, codes, "w1"))
                 if o == 1 and 1 <= step <= T // C:
                     hidden(shared_acc, grouped[:, PACK * C : 2 * PACK * C], SLOTS + (step - 1) * C)
-                if o == 0 and step >= 2 and e - 1 in UNDELAYED:
-                    hidden(acc, fresh_h(), (e - 1) * C)
-                if o == 1 and step >= 2 and e - 1 not in UNDELAYED:
+                if step >= 2 and o == RELU_AFTER_PASS[e - 1]:
                     hidden(acc, grouped[:, : PACK * C], (e - 1) * C)
             if e == SHARED:
                 shared_q = w1_q
@@ -191,7 +194,6 @@ def tile_moe_shr_mlp_relu_kernel(tc, x_words, x_scales, w1, w2, gate, offs, pos1
                 shared_acc = first_layer(shared_q, tok_words, tok_scales, step * C)
             if e != SHARED:
                 acc = first_layer(w1_q, slot_words, slot_scales, (e * C) % GATHER)
-        hidden(acc, fresh_h(), (E - 1) * C)
 
         gate_first = (E + 1) * PACK * N
         last = stream.tile([P, gate_first + 2 * T], F32, name="last", tag="raw", align_bytes=64)
@@ -199,24 +201,25 @@ def tile_moe_shr_mlp_relu_kernel(tc, x_words, x_scales, w1, w2, gate, offs, pos1
         gates = last[:, gate_first:].rearrange("p (r t) -> p r t", t=T)
         for e0, e1 in W2_LOADS:
             nc.sync.dma_start(out=w2_raw[:, e0:e1, :], in_=w2_rows[:, e0:e1, :])
-        for r in range(2):
-            nc.sync.dma_start(out=gates[:, r, :], in_=gate[r])
+        nc.sync.dma_start(out=gates, in_=gate.rearrange("r p t -> p r t"))
         for kind, e0, e1, on_vector in TAIL:
             if kind == "q":
-                quantize_w2(w2_raw, e0, e1)
+                grouped = quantize_w2(w2_raw, e0, e1)
+                if e0 <= LAST_RELU_AFTER < e1:
+                    hidden(acc, grouped[:, 0, :], (E - 1) * C, True)
             else:
                 routed_results(e0, e1, nc.vector.tensor_copy if on_vector else nc.scalar.copy)
 
-        for part, (t0, t1) in enumerate(TOKEN_PARTS):
-            width = t1 - t0
-            ys = psum.tile([P, width], F32, name="ys", tag="bank")
+        first_term = keep.tile([P, T], F32, name="first_term")
+        second_term = keep.tile([P, T], F32, name="second_term")
+        partial = keep.tile([P, T], F32, name="partial")
+        result = keep.tile([P, T], F32, name="result")
+        nc.vector.tensor_tensor(first_term[:], y[:].indirect(pos1_sb[:]), gates[:, 0, :], MULT)
+        nc.vector.tensor_tensor(second_term[:], y[:].indirect(pos2_sb[:]), gates[:, 1, :], MULT)
+        for t0, t1 in TOKEN_PARTS:
+            ys = psum.tile([P, t1 - t0], F32, name="ys", tag="bank")
             second_layer(ys[:], SHARED, slice(SLOTS + t0, SLOTS + t1))
-            first_term = keep.tile([P, width], F32, name="first_term%d" % part)
-            second_term = keep.tile([P, width], F32, name="second_term%d" % part)
-            partial = keep.tile([P, width], F32, name="partial%d" % part)
-            result = keep.tile([P, width], F32, name="result%d" % part)
-            nc.vector.tensor_tensor(first_term[:], y[:].indirect(pos1_sb[:, t0 // 16 : t1 // 16]), gates[:, 0, t0:t1], MULT)
-            nc.vector.tensor_tensor(second_term[:], y[:].indirect(pos2_sb[:, t0 // 16 : t1 // 16]), gates[:, 1, t0:t1], MULT)
-            nc.vector.tensor_tensor(partial[:], first_term[:], second_term[:], ADD)
-            nc.vector.tensor_tensor(result[:], ys[:], partial[:], ADD)
-            nc.sync.dma_start(out=out[:, t0:t1], in_=result[:])
+            nc.vector.tensor_tensor(partial[:, t0:t1], ys[:], first_term[:, t0:t1], ADD)
+        for t0, t1 in TOKEN_PARTS:
+            nc.vector.tensor_tensor(result[:, t0:t1], partial[:, t0:t1], second_term[:, t0:t1], ADD)
+            nc.sync.dma_start(out=out[:, t0:t1], in_=result[:, t0:t1])

@@ -22,13 +22,9 @@ PASSES = K // (P * PACK)
 SLOTS = E * C
 SHARED = E
 GATHER = 256
-WHOLE_LOADS = 9
-RELU_AFTER_PASS = (1, 1, 1, 1, 1, 0, 1, 0, 0)
-LAST_RELU_AFTER = 2
-HALVED = ((9, 0), (9, 1), (9, 2),)
-W2_LOADS = ((0, 2), (2, 3), (3, 4), (4, 6), (6, 7), (7, 8), (8, 10), (10, 11))
-W2_ON_SCALAR = (0, 2, 3, 4, 6, 7, 9, 10,)
-TAIL = (("q", 0, 2, False), ("q", 2, 3, False), ("q", 3, 5, False), ("y", 0, 4, False), ("q", 5, 6, False), ("q", 6, 7, False), ("q", 7, 8, False), ("y", 4, 8, False), ("q", 8, 9, False), ("y", 8, 9, True), ("q", 9, 10, False), ("y", 9, 10, True), ("q", 10, 11, False))
+BY_PASS = 2
+EARLY_W2 = 4
+EARLY_W2_AFTER = 6
 TOKEN_PARTS = ((0, 512), (512, 640))
 
 
@@ -129,27 +125,26 @@ def tile_moe_shr_mlp_relu_kernel(tc, x_words, x_scales, w1, w2, gate, offs, pos1
             h_cols = slice(h_first, h_first + C)
             nc.vector.quantize_mx(out=h_codes[:, h_cols].bitcast(FP8X4), scales=h_scales[:, h_cols], in_=h)
 
-        def quantize_w2(raw, e0, e1):
-            grouped = stage.tile([P, e1 - e0, PACK * N], BF16, name="w2_bf16", bufs=6, align_bytes=64)
-            on_vector = [e for e in range(e0, e1) if e not in W2_ON_SCALAR]
-            for e in range(e0, e1):
-                if e in W2_ON_SCALAR:
-                    nc.scalar.copy(
-                        out=grouped[:, e - e0, :].rearrange("p (c i j) -> p c j i", i=4, j=PACK),
-                        in_=raw[:, e, :].rearrange("p (j c i) -> p c j i", i=4, j=PACK),
-                    )
-            if on_vector:
-                v0, v1 = on_vector[0], on_vector[-1] + 1
-                nc.vector.tensor_copy(
-                    out=grouped[:, v0 - e0 : v1 - e0, :].rearrange("p e (n j) -> p e n j", j=PACK),
-                    in_=raw[:, v0:v1, :].rearrange("p e (j n) -> p e n j", j=PACK),
+        def round_w2(raw, count, on_scalar):
+            grouped = stage.tile([P, count, PACK * N], BF16, name="w2_bf16", bufs=5, align_bytes=64)
+            for i in range(on_scalar):
+                nc.scalar.copy(
+                    out=grouped[:, i, :].rearrange("p (c i j) -> p c j i", i=4, j=PACK),
+                    in_=raw[:, i, :].rearrange("p (j c i) -> p c j i", i=4, j=PACK),
                 )
+            if on_scalar < count:
+                nc.vector.tensor_copy(
+                    out=grouped[:, on_scalar:, :].rearrange("p e (n j) -> p e n j", j=PACK),
+                    in_=raw[:, on_scalar:, :].rearrange("p e (j n) -> p e n j", j=PACK),
+                )
+            return grouped
+
+        def quantize_w2(grouped, e0, e1):
             nc.vector.quantize_mx(
                 out=w2_codes[:, e0 * N : e1 * N].bitcast(FP8X4),
                 scales=w2_scales[:, e0 * N : e1 * N],
                 in_=grouped[:].rearrange("p e w -> p (e w)"),
             )
-            return grouped
 
         def second_layer(acc, e, h_cols):
             nc.tensor.matmul_mx(
@@ -169,7 +164,8 @@ def tile_moe_shr_mlp_relu_kernel(tc, x_words, x_scales, w1, w2, gate, offs, pos1
             copy(out=y[:, e0 * C : e1 * C], in_=acc[:])
 
         for step, e in enumerate([SHARED] + list(range(E))):
-            raw = load_w1(e, step < WHOLE_LOADS)
+            whole = e == SHARED or e < E - BY_PASS
+            raw = load_w1(e, whole)
             if step == 0:
                 load_token_scales()
             if step == 1:
@@ -183,10 +179,10 @@ def tile_moe_shr_mlp_relu_kernel(tc, x_words, x_scales, w1, w2, gate, offs, pos1
                 if e == SHARED:
                     w1_q.append(quantize_w1(grouped, 1, keep, "shared%d" % o))
                 else:
-                    w1_q.append(quantize_w1(grouped, 2 if (e, o) in HALVED else 1, codes, "w1"))
+                    w1_q.append(quantize_w1(grouped, 2 if e == E - 1 else 1, codes, "w1"))
                 if o == 1 and 1 <= step <= T // C:
                     hidden(shared_acc, grouped[:, PACK * C : 2 * PACK * C], SLOTS + (step - 1) * C)
-                if step >= 2 and o == RELU_AFTER_PASS[e - 1]:
+                if step >= 2 and o == (1 if whole else 0):
                     hidden(acc, grouped[:, : PACK * C], (e - 1) * C)
             if e == SHARED:
                 shared_q = w1_q
@@ -194,21 +190,33 @@ def tile_moe_shr_mlp_relu_kernel(tc, x_words, x_scales, w1, w2, gate, offs, pos1
                 shared_acc = first_layer(shared_q, tok_words, tok_scales, step * C)
             if e != SHARED:
                 acc = first_layer(w1_q, slot_words, slot_scales, (e * C) % GATHER)
+            if e == EARLY_W2_AFTER:
+                early = stream.tile([P, EARLY_W2, PACK * N], F32, name="early", tag="raw", align_bytes=64)
+                nc.sync.dma_start(out=early[:], in_=w2_rows[:, :EARLY_W2, :])
+                quantize_w2(round_w2(early, EARLY_W2, EARLY_W2 // 2), 0, EARLY_W2)
+                routed_results(0, EARLY_W2, nc.scalar.copy)
 
         gate_first = (E + 1) * PACK * N
         last = stream.tile([P, gate_first + 2 * T], F32, name="last", tag="raw", align_bytes=64)
         w2_raw = last[:, :gate_first].rearrange("p (e w) -> p e w", w=PACK * N)
         gates = last[:, gate_first:].rearrange("p (r t) -> p r t", t=T)
-        for e0, e1 in W2_LOADS:
+        pairs = [(e, e + 2) for e in range(EARLY_W2, E - 2, 2)]
+        singles = [(e, e + 1) for e in range(E - 2, E)]
+        for e0, e1 in pairs + singles:
             nc.sync.dma_start(out=w2_raw[:, e0:e1, :], in_=w2_rows[:, e0:e1, :])
-        nc.sync.dma_start(out=gates, in_=gate.rearrange("r p t -> p r t"))
-        for kind, e0, e1, on_vector in TAIL:
-            if kind == "q":
-                grouped = quantize_w2(w2_raw, e0, e1)
-                if e0 <= LAST_RELU_AFTER < e1:
-                    hidden(acc, grouped[:, 0, :], (E - 1) * C, True)
-            else:
-                routed_results(e0, e1, nc.vector.tensor_copy if on_vector else nc.scalar.copy)
+        nc.sync.dma_start(out=gates[:, 0, :], in_=gate[0])
+        nc.sync.dma_start(out=w2_raw[:, SHARED, :], in_=w2_rows[:, SHARED, :])
+        nc.sync.dma_start(out=gates[:, 1, :], in_=gate[1])
+
+        h_last = stage.tile([P, PACK * C], BF16, name="h_last", bufs=1, align_bytes=64)
+        hidden(acc, h_last[:], (E - 1) * C)
+        for (e0, e1), on_scalar in zip(pairs, (2, 0)):
+            quantize_w2(round_w2(w2_raw[:, e0:e1, :], 2, on_scalar), e0, e1)
+        routed_results(EARLY_W2, E - 2, nc.scalar.copy)
+        for (e0, e1), on_scalar in zip(singles, (1, 0)):
+            quantize_w2(round_w2(w2_raw[:, e0:e1, :], 1, on_scalar), e0, e1)
+        routed_results(E - 2, E, nc.vector.tensor_copy)
+        quantize_w2(round_w2(w2_raw[:, SHARED : SHARED + 1, :], 1, 1), SHARED, SHARED + 1)
 
         first_term = keep.tile([P, T], F32, name="first_term")
         second_term = keep.tile([P, T], F32, name="second_term")

@@ -23,7 +23,7 @@ SLOTS = E * C
 SHARED = E
 GATHER = 256
 BY_PASS = 2
-EARLY_W2 = 4
+EARLY_W2 = 2
 EARLY_W2_AFTER = 6
 TOKEN_PARTS = ((0, 512), (512, 640))
 
@@ -74,21 +74,22 @@ def tile_moe_shr_mlp_relu_kernel(tc, x_words, x_scales, w1, w2, gate, offs, pos1
                     nc.sync.dma_start(out=raw[:, o, :], in_=w1_rows[e, :, o, :])
             return raw
 
-        def round_w1(raw, o):
+        def round_w1(raw, o, on_scalar):
             grouped = stage.tile([P, PACK * H], BF16, name="w1_bf16", align_bytes=64)
             src = raw[:, o, :].rearrange("p (j m t) -> p m j t", j=PACK, t=PACK)
             dst = grouped[:].rearrange("p (t m j) -> p m j t", j=PACK, t=PACK)
-            nc.scalar.copy(out=dst[:, :, :, :2], in_=src[:, :, :, :2])
+            nc.scalar.copy(out=dst[:, :, :, :on_scalar], in_=src[:, :, :, :on_scalar])
             nc.vector.tensor_copy(out=dst[:, :, :, 2:], in_=src[:, :, :, 2:])
+            if on_scalar < 2:
+                nc.vector.tensor_copy(out=dst[:, :, :, on_scalar:2], in_=src[:, :, :, on_scalar:2])
             return grouped
 
-        def quantize_w1(grouped, calls, pool, name):
+        def quantize_w1(grouped, tile_runs, pool, name):
             w1_codes = pool.tile([P, H], U32, name=name + "_codes", align_bytes=64)
             w1_scales = pool.tile([P, H], U8, name=name + "_scales", align_bytes=64)
-            width = H // calls
-            for first in range(H - width, -1, -width):
-                cols = slice(first, first + width)
-                nc.vector.quantize_mx(out=w1_codes[:, cols].bitcast(FP8X4), scales=w1_scales[:, cols], in_=grouped[:, PACK * first : PACK * (first + width)])
+            for t0, t1 in tile_runs:
+                cols = slice(t0 * P, t1 * P)
+                nc.vector.quantize_mx(out=w1_codes[:, cols].bitcast(FP8X4), scales=w1_scales[:, cols], in_=grouped[:, PACK * t0 * P : PACK * t1 * P])
             return w1_codes, w1_scales
 
         def gather_slots(first):
@@ -104,7 +105,7 @@ def tile_moe_shr_mlp_relu_kernel(tc, x_words, x_scales, w1, w2, gate, offs, pos1
             acc = psum.tile([P, PACK, C], F32, name="acc1", tag="bank")
             cols = slice(first, first + C)
             for o in range(PASSES):
-                for t in reversed(range(PACK)):
+                for t in (3, 2, 0, 1):
                     w1_codes, w1_scales = w1_q[o]
                     nc.tensor.matmul_mx(
                         out=acc[:, t, :],
@@ -113,7 +114,7 @@ def tile_moe_shr_mlp_relu_kernel(tc, x_words, x_scales, w1, w2, gate, offs, pos1
                         rhs=words[:, o, cols].bitcast(FP8X4),
                         rhs_scale=scales[4 * o :, cols],
                         start=(o == 0 and t == PACK - 1),
-                        stop=(o == PASSES - 1 and t == 0),
+                        stop=(o == PASSES - 1 and t == 1),
                     )
             return acc
 
@@ -126,7 +127,7 @@ def tile_moe_shr_mlp_relu_kernel(tc, x_words, x_scales, w1, w2, gate, offs, pos1
             nc.vector.quantize_mx(out=h_codes[:, h_cols].bitcast(FP8X4), scales=h_scales[:, h_cols], in_=h)
 
         def round_w2(raw, count, on_scalar):
-            grouped = stage.tile([P, count, PACK * N], BF16, name="w2_bf16", bufs=5, align_bytes=64)
+            grouped = stage.tile([P, count, PACK * N], BF16, name="w2_bf16", bufs=2, align_bytes=64)
             for i in range(on_scalar):
                 nc.scalar.copy(
                     out=grouped[:, i, :].rearrange("p (c i j) -> p c j i", i=4, j=PACK),
@@ -139,11 +140,17 @@ def tile_moe_shr_mlp_relu_kernel(tc, x_words, x_scales, w1, w2, gate, offs, pos1
                 )
             return grouped
 
+        def round_one(dst, src, on_scalar):
+            if on_scalar:
+                nc.scalar.copy(out=dst.rearrange("p (c i j) -> p c j i", i=4, j=PACK), in_=src.rearrange("p (j c i) -> p c j i", i=4, j=PACK))
+            else:
+                nc.vector.tensor_copy(out=dst.rearrange("p (n j) -> p n j", j=PACK), in_=src.rearrange("p (j n) -> p n j", j=PACK))
+
         def quantize_w2(grouped, e0, e1):
             nc.vector.quantize_mx(
                 out=w2_codes[:, e0 * N : e1 * N].bitcast(FP8X4),
                 scales=w2_scales[:, e0 * N : e1 * N],
-                in_=grouped[:].rearrange("p e w -> p (e w)"),
+                in_=grouped[:, :, :].rearrange("p e w -> p (e w)"),
             )
 
         def second_layer(acc, e, h_cols):
@@ -157,11 +164,11 @@ def tile_moe_shr_mlp_relu_kernel(tc, x_words, x_scales, w1, w2, gate, offs, pos1
                 stop=True,
             )
 
-        def routed_results(e0, e1, copy):
-            acc = psum.tile([P, (e1 - e0) * C], F32, name="acc2", tag="bank")
-            for e in range(e0, e1):
-                second_layer(acc[:, (e - e0) * C : (e - e0 + 1) * C], e, slice(e * C, (e + 1) * C))
-            copy(out=y[:, e0 * C : e1 * C], in_=acc[:])
+        def routed_results(experts, copy):
+            acc = psum.tile([P, len(experts), C], F32, name="acc2", tag="bank")
+            for i, e in enumerate(experts):
+                second_layer(acc[:, i, :], e, slice(e * C, (e + 1) * C))
+            copy(out=y[:].rearrange("p (e c) -> p e c", c=C)[:, experts.start : experts.stop : experts.step, :], in_=acc[:])
 
         for step, e in enumerate([SHARED] + list(range(E))):
             whole = e == SHARED or e < E - BY_PASS
@@ -175,11 +182,12 @@ def tile_moe_shr_mlp_relu_kernel(tc, x_words, x_scales, w1, w2, gate, offs, pos1
                 slot_words, slot_scales = gather_slots(e * C)
             w1_q = []
             for o in range(PASSES):
-                grouped = round_w1(raw, o)
+                closing = e == E - 1 and o == PASSES - 1
+                grouped = round_w1(raw, o, 1 if closing else 2)
                 if e == SHARED:
-                    w1_q.append(quantize_w1(grouped, 1, keep, "shared%d" % o))
+                    w1_q.append(quantize_w1(grouped, [(0, 4)], keep, "shared%d" % o))
                 else:
-                    w1_q.append(quantize_w1(grouped, 2 if e == E - 1 else 1, codes, "w1"))
+                    w1_q.append(quantize_w1(grouped, [(2, 4), (0, 1), (1, 2)] if closing else [(2, 4), (0, 2)] if e == E - 1 else [(0, 4)], codes, "w1"))
                 if o == 1 and 1 <= step <= T // C:
                     hidden(shared_acc, grouped[:, PACK * C : 2 * PACK * C], SLOTS + (step - 1) * C)
                 if step >= 2 and o == (1 if whole else 0):
@@ -193,30 +201,28 @@ def tile_moe_shr_mlp_relu_kernel(tc, x_words, x_scales, w1, w2, gate, offs, pos1
             if e == EARLY_W2_AFTER:
                 early = stream.tile([P, EARLY_W2, PACK * N], F32, name="early", tag="raw", align_bytes=64)
                 nc.sync.dma_start(out=early[:], in_=w2_rows[:, :EARLY_W2, :])
-                quantize_w2(round_w2(early, EARLY_W2, EARLY_W2 // 2), 0, EARLY_W2)
-                routed_results(0, EARLY_W2, nc.scalar.copy)
+                for e0, e1 in ((0, 2),):
+                    quantize_w2(round_w2(early[:, e0:e1, :], e1 - e0, (e1 - e0) // 2), e0, e1)
+                    routed_results(range(e0, e1), nc.scalar.copy)
 
         gate_first = (E + 1) * PACK * N
         last = stream.tile([P, gate_first + 2 * T], F32, name="last", tag="raw", align_bytes=64)
         w2_raw = last[:, :gate_first].rearrange("p (e w) -> p e w", w=PACK * N)
         gates = last[:, gate_first:].rearrange("p (r t) -> p r t", t=T)
-        pairs = [(e, e + 2) for e in range(EARLY_W2, E - 2, 2)]
-        singles = [(e, e + 1) for e in range(E - 2, E)]
-        for e0, e1 in pairs + singles:
-            nc.sync.dma_start(out=w2_raw[:, e0:e1, :], in_=w2_rows[:, e0:e1, :])
-        nc.sync.dma_start(out=gates[:, 0, :], in_=gate[0])
-        nc.sync.dma_start(out=w2_raw[:, SHARED, :], in_=w2_rows[:, SHARED, :])
-        nc.sync.dma_start(out=gates[:, 1, :], in_=gate[1])
+        for e in range(EARLY_W2, E + 1):
+            nc.sync.dma_start(out=w2_raw[:, e, :], in_=w2_rows[:, e, :])
+        for r in range(2):
+            nc.sync.dma_start(out=gates[:, r, :], in_=gate[r])
 
-        h_last = stage.tile([P, PACK * C], BF16, name="h_last", bufs=1, align_bytes=64)
-        hidden(acc, h_last[:], (E - 1) * C)
-        for (e0, e1), on_scalar in zip(pairs, (2, 0)):
-            quantize_w2(round_w2(w2_raw[:, e0:e1, :], 2, on_scalar), e0, e1)
-        routed_results(EARLY_W2, E - 2, nc.scalar.copy)
-        for (e0, e1), on_scalar in zip(singles, (1, 0)):
-            quantize_w2(round_w2(w2_raw[:, e0:e1, :], 1, on_scalar), e0, e1)
-        routed_results(E - 2, E, nc.vector.tensor_copy)
-        quantize_w2(round_w2(w2_raw[:, SHARED : SHARED + 1, :], 1, 1), SHARED, SHARED + 1)
+        late = stage.tile([P, E + 1 - EARLY_W2, PACK * N], BF16, name="late", bufs=1, align_bytes=64)
+        for e in range(EARLY_W2, E + 1):
+            if e == 4 + 1:
+                hidden(acc, w2_raw[:, 4, : PACK * C // 2].bitcast(BF16), (E - 1) * C)
+            round_one(late[:, e - EARLY_W2, :], w2_raw[:, e, :], e in (2, 3, 4, 6, 8, 10))
+        for e0, e1 in ((2, 4), (4, 6), (6, 8), (8, 9), (9, 10), (10, 11)):
+            quantize_w2(late[:, e0 - EARLY_W2 : e1 - EARLY_W2, :], e0, e1)
+        for experts, s in ((range(2, 4), 1), (range(5, 9), 1), (range(4, 10, 5), 0)):
+            routed_results(experts, nc.scalar.copy if s else nc.vector.tensor_copy)
 
         first_term = keep.tile([P, T], F32, name="first_term")
         second_term = keep.tile([P, T], F32, name="second_term")

@@ -1,6 +1,7 @@
 from contextlib import ExitStack
 
 import concourse.mybir as mybir
+from concourse.masks import make_identity
 
 K, T, E, C, H, N = 1536, 640, 10, 128, 512, 128
 FLOPS = 2 * (E * C + T) * (K * H + H * N)
@@ -26,6 +27,26 @@ BY_PASS = 2
 EARLY_W2 = 2
 EARLY_W2_AFTER = 6
 TOKEN_PARTS = ((0, 512), (512, 640))
+SMALL_Q = 'gpsimd'
+LATE_LOADS = ((2, 3), (3, 4), (4, 5), (5, 6), (6, 7), (7, 8), (8, 9), (9, 10))
+W1_LOADS = {8: ((0, 2), (2, 3)), 9: ((0, 1), (1, 2), (2, 3))}
+RELU_AT = {8: 0, 9: 0}
+ON_S = (2, 3, 4, 6, 8)
+QUANT = ((2, 4), (4, 6), (6, 7), (7, 8), (8, 9), (9, 10), (10, 11))
+RESULTS = ((range(2, 4), 1), (range(4, 8), 1), (range(8, 9), 1), (range(9, 10), 1))
+HOLD = 4
+POS_LATE = True
+G2_PARTS = ((0, 320), (320, 640))
+ADDS = (('p', 0, 0, 256), ('p', 0, 256, 512), ('r', 0, 0, 256), ('p', 0, 512, 640), ('r', 1, 256, 512), ('r', 2, 512, 640))
+STORE_Q = 'sss'
+HOLD_PARTIAL = True
+PE_PARTS = ((0, 256), (256, 512), (512, 640))
+V_PARTS = ()
+SEQ = (('f', 0), ('b', 0), ('f', 1), ('f', 2), ('b', 1), ('b', 2))
+WARM1 = 512
+WARM2 = 256
+G1_PARTS = ((0, 256), (256, 512), (512, 640))
+YS_PARTS = ((0, 256), (256, 640))
 
 
 def tile_moe_shr_mlp_relu_kernel(tc, x_words, x_scales, w1, w2, gate, offs, pos1, pos2, out):
@@ -52,26 +73,26 @@ def tile_moe_shr_mlp_relu_kernel(tc, x_words, x_scales, w1, w2, gate, offs, pos1
         w1_rows = w1.rearrange("e (o p j) c -> e p o (j c)", p=P, j=PACK)
         w2_rows = w2.rearrange("e (p j) n -> p e (j n)", j=PACK)
 
-        scale_rows = keep.tile([P, T // 4], I32, name="scale_rows", align_bytes=64)
-
         def load_token_scales():
             nc.gpsimd.memset(tok_scales[:], 0)
             scale_words = x_scales.bitcast(I32)
+            if SMALL_Q == 'sync':
+                scale_rows = keep.tile([P, T // 4], I32, name="scale_rows", align_bytes=64)
             for q in range(4):
                 live = slice(32 * q, 32 * q + 4 * PASSES)
-                nc.sync.dma_start(out=scale_rows[live, :], in_=scale_words[:, 4 * q : 4 * q + 4, :])
-                nc.gpsimd.tensor_copy(out=tok_scales[live, :].bitcast(I32), in_=scale_rows[live, :])
+                if SMALL_Q == 'sync':
+                    nc.sync.dma_start(out=scale_rows[live, :], in_=scale_words[:, 4 * q : 4 * q + 4, :])
+                    nc.gpsimd.tensor_copy(out=tok_scales[live, :].bitcast(I32), in_=scale_rows[live, :])
+                else:
+                    nc.gpsimd.dma_start(out=tok_scales[live, :].bitcast(I32), in_=scale_words[:, 4 * q : 4 * q + 4, :])
 
         nc.sync.dma_start(out=tok_words[:], in_=x_words.rearrange("o p t r -> p o (t r)").bitcast(I32))
         nc.sync.dma_start(offs_sb[:], offs)
 
         def load_w1(e, whole):
             raw = stream.tile([P, PASSES, PACK * H], F32, name="raw", tag="raw", align_bytes=64)
-            if whole:
-                nc.sync.dma_start(out=raw[:], in_=w1_rows[e])
-            else:
-                for o in range(PASSES):
-                    nc.sync.dma_start(out=raw[:, o, :], in_=w1_rows[e, :, o, :])
+            for o0, o1 in W1_LOADS.get(e, ((0, PASSES),)):
+                nc.sync.dma_start(out=raw[:, o0:o1, :], in_=w1_rows[e, :, o0:o1, :])
             return raw
 
         def round_w1(raw, o, on_scalar):
@@ -175,7 +196,7 @@ def tile_moe_shr_mlp_relu_kernel(tc, x_words, x_scales, w1, w2, gate, offs, pos1
             raw = load_w1(e, whole)
             if step == 0:
                 load_token_scales()
-            if step == 1:
+            if step == 1 and not POS_LATE:
                 nc.sync.dma_start(pos1_sb[:], pos1)
                 nc.sync.dma_start(pos2_sb[:], pos2)
             if e != SHARED and (e * C) % GATHER == 0:
@@ -190,7 +211,7 @@ def tile_moe_shr_mlp_relu_kernel(tc, x_words, x_scales, w1, w2, gate, offs, pos1
                     w1_q.append(quantize_w1(grouped, [(2, 4), (0, 1), (1, 2)] if closing else [(2, 4), (0, 2)] if e == E - 1 else [(0, 4)], codes, "w1"))
                 if o == 1 and 1 <= step <= T // C:
                     hidden(shared_acc, grouped[:, PACK * C : 2 * PACK * C], SLOTS + (step - 1) * C)
-                if step >= 2 and o == (1 if whole else 0):
+                if step >= 2 and o == RELU_AT.get(e, 1):
                     hidden(acc, grouped[:, : PACK * C], (e - 1) * C)
             if e == SHARED:
                 shared_q = w1_q
@@ -201,7 +222,7 @@ def tile_moe_shr_mlp_relu_kernel(tc, x_words, x_scales, w1, w2, gate, offs, pos1
             if e == EARLY_W2_AFTER:
                 early = stream.tile([P, EARLY_W2, PACK * N], F32, name="early", tag="raw", align_bytes=64)
                 nc.sync.dma_start(out=early[:], in_=w2_rows[:, :EARLY_W2, :])
-                for e0, e1 in ((0, 2),):
+                for e0, e1 in [(i, min(i + 2, EARLY_W2)) for i in range(0, EARLY_W2, 2)]:
                     quantize_w2(round_w2(early[:, e0:e1, :], e1 - e0, (e1 - e0) // 2), e0, e1)
                     routed_results(range(e0, e1), nc.scalar.copy)
 
@@ -209,31 +230,76 @@ def tile_moe_shr_mlp_relu_kernel(tc, x_words, x_scales, w1, w2, gate, offs, pos1
         last = stream.tile([P, gate_first + 2 * T], F32, name="last", tag="raw", align_bytes=64)
         w2_raw = last[:, :gate_first].rearrange("p (e w) -> p e w", w=PACK * N)
         gates = last[:, gate_first:].rearrange("p (r t) -> p r t", t=T)
-        for e in range(EARLY_W2, E + 1):
-            nc.sync.dma_start(out=w2_raw[:, e, :], in_=w2_rows[:, e, :])
-        for r in range(2):
+        for e0, e1 in LATE_LOADS + ((E, E + 1),):
+            nc.sync.dma_start(out=w2_raw[:, e0:e1, :], in_=w2_rows[:, e0:e1, :])
+        for r, (pos_sb, pos) in enumerate(((pos1_sb, pos1), (pos2_sb, pos2))):
+            if POS_LATE:
+                nc.sync.dma_start(pos_sb[:], pos)
             nc.sync.dma_start(out=gates[:, r, :], in_=gate[r])
 
         late = stage.tile([P, E + 1 - EARLY_W2, PACK * N], BF16, name="late", bufs=1, align_bytes=64)
         for e in range(EARLY_W2, E + 1):
-            if e == 4 + 1:
-                hidden(acc, w2_raw[:, 4, : PACK * C // 2].bitcast(BF16), (E - 1) * C)
-            round_one(late[:, e - EARLY_W2, :], w2_raw[:, e, :], e in (2, 3, 4, 6, 8, 10))
-        for e0, e1 in ((2, 4), (4, 6), (6, 8), (8, 9), (9, 10), (10, 11)):
+            if e == HOLD + 1:
+                hidden(acc, w2_raw[:, HOLD, : PACK * C // 2].bitcast(BF16), (E - 1) * C)
+            round_one(late[:, e - EARLY_W2, :], w2_raw[:, e, :], e in ON_S)
+        for e0, e1 in QUANT:
             quantize_w2(late[:, e0 - EARLY_W2 : e1 - EARLY_W2, :], e0, e1)
-        for experts, s in ((range(2, 4), 1), (range(5, 9), 1), (range(4, 10, 5), 0)):
+        for experts, s in RESULTS:
             routed_results(experts, nc.scalar.copy if s else nc.vector.tensor_copy)
 
         first_term = keep.tile([P, T], F32, name="first_term")
         second_term = keep.tile([P, T], F32, name="second_term")
-        partial = keep.tile([P, T], F32, name="partial")
         result = keep.tile([P, T], F32, name="result")
-        nc.vector.tensor_tensor(first_term[:], y[:].indirect(pos1_sb[:]), gates[:, 0, :], MULT)
-        nc.vector.tensor_tensor(second_term[:], y[:].indirect(pos2_sb[:]), gates[:, 1, :], MULT)
-        for t0, t1 in TOKEN_PARTS:
+        shared_turned = keep.tile([P, T], F32, name="shared_turned")
+        first_turned = keep.tile([P, T], F32, name="first_turned")
+        identity = keep.tile([P, P], F32, name="identity")
+        make_identity(nc, identity[:])
+        for t0, t1 in G1_PARTS:
+            nc.vector.tensor_tensor(first_term[:, t0:t1], y[:].indirect(pos1_sb[:, t0 // 16 : t1 // 16]), gates[:, 0, t0:t1], MULT)
+        for t0, t1 in V_PARTS:
             ys = psum.tile([P, t1 - t0], F32, name="ys", tag="bank")
             second_layer(ys[:], SHARED, slice(SLOTS + t0, SLOTS + t1))
-            nc.vector.tensor_tensor(partial[:, t0:t1], ys[:], first_term[:, t0:t1], ADD)
-        for t0, t1 in TOKEN_PARTS:
-            nc.vector.tensor_tensor(result[:, t0:t1], partial[:, t0:t1], second_term[:, t0:t1], ADD)
+            nc.vector.tensor_tensor(first_turned[:, t0:t1], ys[:], first_term[:, t0:t1], ADD)
+        for t0, t1 in G2_PARTS:
+            nc.vector.tensor_tensor(second_term[:, t0:t1], y[:].indirect(pos2_sb[:, t0 // 16 : t1 // 16]), gates[:, 1, t0:t1], MULT)
+        def warm_up(e, width):
+            idle = psum.tile([P, width], F32, name="idle", tag="bank")
+            second_layer(idle[:], e, slice(0, width))
+
+        if WARM1:
+            warm_up(E - 1, WARM1)
+        for t0, t1 in YS_PARTS:
+            ys = psum.tile([P, t1 - t0], F32, name="ys", tag="bank")
+            for b in range(t0, t1, P):
+                cols = slice(SLOTS + b, SLOTS + b + P)
+                nc.tensor.matmul_mx(
+                    out=ys[:, b - t0 : b - t0 + P],
+                    lhsT=h_codes[:, cols].bitcast(FP8X4),
+                    lhsT_scale=h_scales[:, cols],
+                    rhs=w2_codes[:, SHARED * N :].bitcast(FP8X4),
+                    rhs_scale=w2_scales[:, SHARED * N :],
+                    start=True,
+                    stop=True,
+                )
+            nc.scalar.copy(out=shared_turned[:, t0:t1], in_=ys[:])
+        if WARM2:
+            warm_up(SHARED, WARM2)
+        for t0, t1 in V_PARTS:
+            nc.vector.tensor_tensor(result[:, t0:t1], first_turned[:, t0:t1], second_term[:, t0:t1], ADD)
             nc.sync.dma_start(out=out[:, t0:t1], in_=result[:, t0:t1])
+        def forth(t0, t1):
+            turned = psum.tile([P, t1 - t0], F32, name="turned", tag="bank")
+            for b in range(t0, t1, P):
+                nc.tensor.transpose(turned[:, b - t0 : b - t0 + P], first_term[:, b : b + P], identity[:])
+            nc.scalar.copy(out=first_turned[:, t0:t1], in_=turned[:])
+
+        def back(t0, t1):
+            partial = psum.tile([P, t1 - t0], F32, name="partial", tag="bank")
+            for i, term in enumerate((shared_turned, first_turned)):
+                for b in range(t0, t1, P):
+                    nc.tensor.matmul(partial[:, b - t0 : b - t0 + P], term[:, b : b + P], identity[:], start=i == 0 and b == t0, stop=i == 1 and b + P == t1, is_transpose=True)
+            nc.vector.tensor_tensor(result[:, t0:t1], partial[:], second_term[:, t0:t1], ADD)
+            nc.sync.dma_start(out=out[:, t0:t1], in_=result[:, t0:t1])
+
+        for kind, i in SEQ:
+            (forth if kind == 'f' else back)(*PE_PARTS[i])

@@ -22,31 +22,22 @@ PACK = 4
 PASSES = K // (P * PACK)
 SLOTS = E * C
 SHARED = E
-GATHER = 256
-BY_PASS = 2
+LAST = E - 1
+PER_COLUMN = 16
+QUADRANT = 32
+SCALE_ROWS = 4
+TOKEN_BLOCKS = T // C
+GATHER = 2 * C
+HALF = PACK // 2
+TILE_ORDER = (3, 2, 0, 1)
+EXPERTS_A_BANK = 4
+
 EARLY_W2 = 2
-EARLY_W2_AFTER = 6
-TOKEN_PARTS = ((0, 512), (512, 640))
-SMALL_Q = 'gpsimd'
-LATE_LOADS = ((2, 3), (3, 4), (4, 5), (5, 6), (6, 7), (7, 8), (8, 9), (9, 10))
-W1_LOADS = {8: ((0, 2), (2, 3)), 9: ((0, 1), (1, 2), (2, 3))}
-RELU_AT = {8: 0, 9: 0}
-ON_S = (2, 3, 4, 6, 8)
-QUANT = ((2, 4), (4, 6), (6, 7), (7, 8), (8, 9), (9, 10), (10, 11))
-RESULTS = ((range(2, 4), 1), (range(4, 8), 1), (range(8, 9), 1), (range(9, 10), 1))
-HOLD = 4
-POS_LATE = True
-G2_PARTS = ((0, 320), (320, 640))
-ADDS = (('p', 0, 0, 256), ('p', 0, 256, 512), ('r', 0, 0, 256), ('p', 0, 512, 640), ('r', 1, 256, 512), ('r', 2, 512, 640))
-STORE_Q = 'sss'
-HOLD_PARTIAL = True
-PE_PARTS = ((0, 256), (256, 512), (512, 640))
-V_PARTS = ()
-SEQ = (('f', 0), ('b', 0), ('f', 1), ('f', 2), ('b', 1), ('b', 2))
-WARM1 = 512
-WARM2 = 256
-G1_PARTS = ((0, 256), (256, 512), (512, 640))
-YS_PARTS = ((0, 256), (256, 640))
+EARLY_AFTER = 6
+SCALAR_RUN = 3
+SINGLY_FROM = 6
+PART = 256
+PARTS = [(t0, min(t0 + PART, T)) for t0 in range(0, T, PART)]
 
 
 def tile_moe_shr_mlp_relu_kernel(tc, x_words, x_scales, w1, w2, gate, offs, pos1, pos2, out):
@@ -54,14 +45,14 @@ def tile_moe_shr_mlp_relu_kernel(tc, x_words, x_scales, w1, w2, gate, offs, pos1
     with ExitStack() as ctx:
         keep = ctx.enter_context(tc.tile_pool(name="keep", bufs=1))
         stream = ctx.enter_context(tc.tile_pool(name="stream", bufs=4))
-        stage = ctx.enter_context(tc.tile_pool(name="stage", bufs=6))
-        gathered = ctx.enter_context(tc.tile_pool(name="gathered", bufs=5))
-        codes = ctx.enter_context(tc.tile_pool(name="codes", bufs=7))
+        stage = ctx.enter_context(tc.tile_pool(name="stage", bufs=2 * PASSES))
+        gathered = ctx.enter_context(tc.tile_pool(name="gathered", bufs=SLOTS // GATHER))
+        codes = ctx.enter_context(tc.tile_pool(name="codes", bufs=2 * PASSES + 1))
         psum = ctx.enter_context(tc.psum_pool(name="psum", bufs=8))
 
-        offs_sb = keep.tile([P, SLOTS // 16], U16, name="offs_sb")
-        pos1_sb = keep.tile([P, T // 16], U16, name="pos1_sb")
-        pos2_sb = keep.tile([P, T // 16], U16, name="pos2_sb")
+        offs_sb = keep.tile([P, SLOTS // PER_COLUMN], U16, name="offs_sb")
+        pos1_sb = keep.tile([P, T // PER_COLUMN], U16, name="pos1_sb")
+        pos2_sb = keep.tile([P, T // PER_COLUMN], U16, name="pos2_sb")
         tok_words = keep.tile([P, PASSES, T], I32, name="tok_words", align_bytes=64)
         tok_scales = keep.tile([P, T], U8, name="tok_scales", align_bytes=64)
         h_codes = keep.tile([P, SLOTS + T], U32, name="h_codes", align_bytes=64)
@@ -76,22 +67,19 @@ def tile_moe_shr_mlp_relu_kernel(tc, x_words, x_scales, w1, w2, gate, offs, pos1
         def load_token_scales():
             nc.gpsimd.memset(tok_scales[:], 0)
             scale_words = x_scales.bitcast(I32)
-            if SMALL_Q == 'sync':
-                scale_rows = keep.tile([P, T // 4], I32, name="scale_rows", align_bytes=64)
-            for q in range(4):
-                live = slice(32 * q, 32 * q + 4 * PASSES)
-                if SMALL_Q == 'sync':
-                    nc.sync.dma_start(out=scale_rows[live, :], in_=scale_words[:, 4 * q : 4 * q + 4, :])
-                    nc.gpsimd.tensor_copy(out=tok_scales[live, :].bitcast(I32), in_=scale_rows[live, :])
-                else:
-                    nc.gpsimd.dma_start(out=tok_scales[live, :].bitcast(I32), in_=scale_words[:, 4 * q : 4 * q + 4, :])
+            for q in range(P // QUADRANT):
+                live = slice(QUADRANT * q, QUADRANT * q + SCALE_ROWS * PASSES)
+                nc.gpsimd.dma_start(out=tok_scales[live, :].bitcast(I32), in_=scale_words[:, SCALE_ROWS * q : SCALE_ROWS * (q + 1), :])
 
-        nc.sync.dma_start(out=tok_words[:], in_=x_words.rearrange("o p t r -> p o (t r)").bitcast(I32))
-        nc.sync.dma_start(offs_sb[:], offs)
-
-        def load_w1(e, whole):
+        def load_w1(e):
+            if e == LAST:
+                cuts = list(range(PASSES + 1))
+            elif e == LAST - 1:
+                cuts = [0, PASSES - 1, PASSES]
+            else:
+                cuts = [0, PASSES]
             raw = stream.tile([P, PASSES, PACK * H], F32, name="raw", tag="raw", align_bytes=64)
-            for o0, o1 in W1_LOADS.get(e, ((0, PASSES),)):
+            for o0, o1 in zip(cuts, cuts[1:]):
                 nc.sync.dma_start(out=raw[:, o0:o1, :], in_=w1_rows[e, :, o0:o1, :])
             return raw
 
@@ -100,23 +88,27 @@ def tile_moe_shr_mlp_relu_kernel(tc, x_words, x_scales, w1, w2, gate, offs, pos1
             src = raw[:, o, :].rearrange("p (j m t) -> p m j t", j=PACK, t=PACK)
             dst = grouped[:].rearrange("p (t m j) -> p m j t", j=PACK, t=PACK)
             nc.scalar.copy(out=dst[:, :, :, :on_scalar], in_=src[:, :, :, :on_scalar])
-            nc.vector.tensor_copy(out=dst[:, :, :, 2:], in_=src[:, :, :, 2:])
-            if on_scalar < 2:
-                nc.vector.tensor_copy(out=dst[:, :, :, on_scalar:2], in_=src[:, :, :, on_scalar:2])
+            nc.vector.tensor_copy(out=dst[:, :, :, HALF:], in_=src[:, :, :, HALF:])
+            if on_scalar < HALF:
+                nc.vector.tensor_copy(out=dst[:, :, :, on_scalar:HALF], in_=src[:, :, :, on_scalar:HALF])
             return grouped
 
         def quantize_w1(grouped, tile_runs, pool, name):
             w1_codes = pool.tile([P, H], U32, name=name + "_codes", align_bytes=64)
             w1_scales = pool.tile([P, H], U8, name=name + "_scales", align_bytes=64)
-            for t0, t1 in tile_runs:
-                cols = slice(t0 * P, t1 * P)
-                nc.vector.quantize_mx(out=w1_codes[:, cols].bitcast(FP8X4), scales=w1_scales[:, cols], in_=grouped[:, PACK * t0 * P : PACK * t1 * P])
+            for tile0, tile1 in tile_runs:
+                cols = slice(tile0 * P, tile1 * P)
+                nc.vector.quantize_mx(
+                    out=w1_codes[:, cols].bitcast(FP8X4),
+                    scales=w1_scales[:, cols],
+                    in_=grouped[:, PACK * tile0 * P : PACK * tile1 * P],
+                )
             return w1_codes, w1_scales
 
         def gather_slots(first):
             slot_words = gathered.tile([P, PASSES, GATHER], U32, name="slot_words", align_bytes=64)
             slot_scales = gathered.tile([P, GATHER], U8, name="slot_scales", align_bytes=64)
-            listed = offs_sb[:, first // 16 : (first + GATHER) // 16]
+            listed = offs_sb[:, first // PER_COLUMN : (first + GATHER) // PER_COLUMN]
             for o in range(PASSES):
                 nc.vector.tensor_copy(slot_words[:, o, :], tok_words[:, o, :].bitcast(U32).indirect(listed))
             nc.vector.tensor_copy(slot_scales[:], tok_scales[:].indirect(listed))
@@ -126,44 +118,30 @@ def tile_moe_shr_mlp_relu_kernel(tc, x_words, x_scales, w1, w2, gate, offs, pos1
             acc = psum.tile([P, PACK, C], F32, name="acc1", tag="bank")
             cols = slice(first, first + C)
             for o in range(PASSES):
-                for t in (3, 2, 0, 1):
-                    w1_codes, w1_scales = w1_q[o]
+                w1_codes, w1_scales = w1_q[o]
+                for t in TILE_ORDER:
                     nc.tensor.matmul_mx(
                         out=acc[:, t, :],
                         lhsT=w1_codes[:, t * P : (t + 1) * P].bitcast(FP8X4),
                         lhsT_scale=w1_scales[:, t * P : (t + 1) * P],
                         rhs=words[:, o, cols].bitcast(FP8X4),
-                        rhs_scale=scales[4 * o :, cols],
-                        start=(o == 0 and t == PACK - 1),
-                        stop=(o == PASSES - 1 and t == 1),
+                        rhs_scale=scales[SCALE_ROWS * o :, cols],
+                        start=(o == 0 and t == TILE_ORDER[0]),
+                        stop=(o == PASSES - 1 and t == TILE_ORDER[-1]),
                     )
             return acc
 
-        def hidden(acc, h, h_first, on_vector=False):
-            if on_vector:
-                nc.vector.tensor_scalar_max(h.rearrange("p (c t) -> p c t", t=PACK), acc[:].rearrange("p t c -> p c t"), 0.0)
-            else:
-                nc.scalar.activation(h.rearrange("p (c t) -> p c t", t=PACK), acc[:].rearrange("p t c -> p c t"), RELU)
+        def hidden(acc, h, h_first):
+            nc.scalar.activation(h.rearrange("p (c t) -> p c t", t=PACK), acc[:].rearrange("p t c -> p c t"), RELU)
             h_cols = slice(h_first, h_first + C)
             nc.vector.quantize_mx(out=h_codes[:, h_cols].bitcast(FP8X4), scales=h_scales[:, h_cols], in_=h)
 
-        def round_w2(raw, count, on_scalar):
-            grouped = stage.tile([P, count, PACK * N], BF16, name="w2_bf16", bufs=2, align_bytes=64)
-            for i in range(on_scalar):
-                nc.scalar.copy(
-                    out=grouped[:, i, :].rearrange("p (c i j) -> p c j i", i=4, j=PACK),
-                    in_=raw[:, i, :].rearrange("p (j c i) -> p c j i", i=4, j=PACK),
-                )
-            if on_scalar < count:
-                nc.vector.tensor_copy(
-                    out=grouped[:, on_scalar:, :].rearrange("p e (n j) -> p e n j", j=PACK),
-                    in_=raw[:, on_scalar:, :].rearrange("p e (j n) -> p e n j", j=PACK),
-                )
-            return grouped
-
-        def round_one(dst, src, on_scalar):
+        def round_w2(dst, src, on_scalar):
             if on_scalar:
-                nc.scalar.copy(out=dst.rearrange("p (c i j) -> p c j i", i=4, j=PACK), in_=src.rearrange("p (j c i) -> p c j i", i=4, j=PACK))
+                nc.scalar.copy(
+                    out=dst.rearrange("p (c i j) -> p c j i", i=PACK, j=PACK),
+                    in_=src.rearrange("p (j c i) -> p c j i", i=PACK, j=PACK),
+                )
             else:
                 nc.vector.tensor_copy(out=dst.rearrange("p (n j) -> p n j", j=PACK), in_=src.rearrange("p (j n) -> p n j", j=PACK))
 
@@ -171,7 +149,7 @@ def tile_moe_shr_mlp_relu_kernel(tc, x_words, x_scales, w1, w2, gate, offs, pos1
             nc.vector.quantize_mx(
                 out=w2_codes[:, e0 * N : e1 * N].bitcast(FP8X4),
                 scales=w2_scales[:, e0 * N : e1 * N],
-                in_=grouped[:, :, :].rearrange("p e w -> p (e w)"),
+                in_=grouped.rearrange("p e w -> p (e w)"),
             )
 
         def second_layer(acc, e, h_cols):
@@ -185,67 +163,79 @@ def tile_moe_shr_mlp_relu_kernel(tc, x_words, x_scales, w1, w2, gate, offs, pos1
                 stop=True,
             )
 
-        def routed_results(experts, copy):
-            acc = psum.tile([P, len(experts), C], F32, name="acc2", tag="bank")
-            for i, e in enumerate(experts):
-                second_layer(acc[:, i, :], e, slice(e * C, (e + 1) * C))
-            copy(out=y[:].rearrange("p (e c) -> p e c", c=C)[:, experts.start : experts.stop : experts.step, :], in_=acc[:])
+        def routed_results(e0, e1):
+            acc = psum.tile([P, e1 - e0, C], F32, name="acc2", tag="bank")
+            for e in range(e0, e1):
+                second_layer(acc[:, e - e0, :], e, slice(e * C, (e + 1) * C))
+            nc.scalar.copy(out=y[:].rearrange("p (e c) -> p e c", c=C)[:, e0:e1, :], in_=acc[:])
+
+        nc.sync.dma_start(out=tok_words[:], in_=x_words.rearrange("o p t r -> p o (t r)").bitcast(I32))
+        nc.sync.dma_start(offs_sb[:], offs)
 
         for step, e in enumerate([SHARED] + list(range(E))):
-            whole = e == SHARED or e < E - BY_PASS
-            raw = load_w1(e, whole)
+            raw = load_w1(e)
             if step == 0:
                 load_token_scales()
-            if step == 1 and not POS_LATE:
-                nc.sync.dma_start(pos1_sb[:], pos1)
-                nc.sync.dma_start(pos2_sb[:], pos2)
             if e != SHARED and (e * C) % GATHER == 0:
                 slot_words, slot_scales = gather_slots(e * C)
+            relu_pass = 0 if e in (LAST - 1, LAST) else 1
             w1_q = []
             for o in range(PASSES):
-                closing = e == E - 1 and o == PASSES - 1
-                grouped = round_w1(raw, o, 1 if closing else 2)
+                closing = e == LAST and o == PASSES - 1
+                grouped = round_w1(raw, o, 1 if closing else HALF)
                 if e == SHARED:
-                    w1_q.append(quantize_w1(grouped, [(0, 4)], keep, "shared%d" % o))
+                    w1_q.append(quantize_w1(grouped, [(0, PACK)], keep, "shared%d" % o))
                 else:
-                    w1_q.append(quantize_w1(grouped, [(2, 4), (0, 1), (1, 2)] if closing else [(2, 4), (0, 2)] if e == E - 1 else [(0, 4)], codes, "w1"))
-                if o == 1 and 1 <= step <= T // C:
+                    if closing:
+                        tile_runs = [(HALF, PACK), (0, 1), (1, HALF)]
+                    elif e == LAST:
+                        tile_runs = [(HALF, PACK), (0, HALF)]
+                    else:
+                        tile_runs = [(0, PACK)]
+                    w1_q.append(quantize_w1(grouped, tile_runs, codes, "w1"))
+                if o == 1 and 1 <= step <= TOKEN_BLOCKS:
                     hidden(shared_acc, grouped[:, PACK * C : 2 * PACK * C], SLOTS + (step - 1) * C)
-                if step >= 2 and o == RELU_AT.get(e, 1):
+                if o == relu_pass and 1 <= e <= LAST:
                     hidden(acc, grouped[:, : PACK * C], (e - 1) * C)
             if e == SHARED:
                 shared_q = w1_q
-            if step < T // C:
+            if step < TOKEN_BLOCKS:
                 shared_acc = first_layer(shared_q, tok_words, tok_scales, step * C)
             if e != SHARED:
                 acc = first_layer(w1_q, slot_words, slot_scales, (e * C) % GATHER)
-            if e == EARLY_W2_AFTER:
+            if e == EARLY_AFTER:
                 early = stream.tile([P, EARLY_W2, PACK * N], F32, name="early", tag="raw", align_bytes=64)
                 nc.sync.dma_start(out=early[:], in_=w2_rows[:, :EARLY_W2, :])
-                for e0, e1 in [(i, min(i + 2, EARLY_W2)) for i in range(0, EARLY_W2, 2)]:
-                    quantize_w2(round_w2(early[:, e0:e1, :], e1 - e0, (e1 - e0) // 2), e0, e1)
-                    routed_results(range(e0, e1), nc.scalar.copy)
+                early_bf16 = stage.tile([P, EARLY_W2, PACK * N], BF16, name="w2_bf16", bufs=2, align_bytes=64)
+                for i in range(EARLY_W2):
+                    round_w2(early_bf16[:, i, :], early[:, i, :], i % 2 == 0)
+                quantize_w2(early_bf16[:], 0, EARLY_W2)
+                routed_results(0, EARLY_W2)
 
         gate_first = (E + 1) * PACK * N
         last = stream.tile([P, gate_first + 2 * T], F32, name="last", tag="raw", align_bytes=64)
         w2_raw = last[:, :gate_first].rearrange("p (e w) -> p e w", w=PACK * N)
         gates = last[:, gate_first:].rearrange("p (r t) -> p r t", t=T)
-        for e0, e1 in LATE_LOADS + ((E, E + 1),):
-            nc.sync.dma_start(out=w2_raw[:, e0:e1, :], in_=w2_rows[:, e0:e1, :])
+        for e in range(EARLY_W2, E + 1):
+            nc.sync.dma_start(out=w2_raw[:, e : e + 1, :], in_=w2_rows[:, e : e + 1, :])
         for r, (pos_sb, pos) in enumerate(((pos1_sb, pos1), (pos2_sb, pos2))):
-            if POS_LATE:
-                nc.sync.dma_start(pos_sb[:], pos)
+            nc.sync.dma_start(pos_sb[:], pos)
             nc.sync.dma_start(out=gates[:, r, :], in_=gate[r])
 
         late = stage.tile([P, E + 1 - EARLY_W2, PACK * N], BF16, name="late", bufs=1, align_bytes=64)
+        run_end = EARLY_W2 + SCALAR_RUN
         for e in range(EARLY_W2, E + 1):
-            if e == HOLD + 1:
-                hidden(acc, w2_raw[:, HOLD, : PACK * C // 2].bitcast(BF16), (E - 1) * C)
-            round_one(late[:, e - EARLY_W2, :], w2_raw[:, e, :], e in ON_S)
-        for e0, e1 in QUANT:
+            if e == run_end:
+                hidden(acc, w2_raw[:, run_end - 1, : PACK * C // 2].bitcast(BF16), LAST * C)
+            on_scalar = e < run_end or (e != SHARED and (e - run_end) % 2 == 1)
+            round_w2(late[:, e - EARLY_W2, :], w2_raw[:, e, :], on_scalar)
+        cuts = list(range(EARLY_W2, SINGLY_FROM, 2)) + list(range(SINGLY_FROM, E + 2))
+        for e0, e1 in zip(cuts, cuts[1:]):
             quantize_w2(late[:, e0 - EARLY_W2 : e1 - EARLY_W2, :], e0, e1)
-        for experts, s in RESULTS:
-            routed_results(experts, nc.scalar.copy if s else nc.vector.tensor_copy)
+        full_banks = E - E % EXPERTS_A_BANK
+        cuts = [EARLY_W2] + list(range(EXPERTS_A_BANK, full_banks, EXPERTS_A_BANK)) + list(range(full_banks, E + 1))
+        for e0, e1 in zip(cuts, cuts[1:]):
+            routed_results(e0, e1)
 
         first_term = keep.tile([P, T], F32, name="first_term")
         second_term = keep.tile([P, T], F32, name="second_term")
@@ -254,21 +244,12 @@ def tile_moe_shr_mlp_relu_kernel(tc, x_words, x_scales, w1, w2, gate, offs, pos1
         first_turned = keep.tile([P, T], F32, name="first_turned")
         identity = keep.tile([P, P], F32, name="identity")
         make_identity(nc, identity[:])
-        for t0, t1 in G1_PARTS:
-            nc.vector.tensor_tensor(first_term[:, t0:t1], y[:].indirect(pos1_sb[:, t0 // 16 : t1 // 16]), gates[:, 0, t0:t1], MULT)
-        for t0, t1 in V_PARTS:
-            ys = psum.tile([P, t1 - t0], F32, name="ys", tag="bank")
-            second_layer(ys[:], SHARED, slice(SLOTS + t0, SLOTS + t1))
-            nc.vector.tensor_tensor(first_turned[:, t0:t1], ys[:], first_term[:, t0:t1], ADD)
-        for t0, t1 in G2_PARTS:
-            nc.vector.tensor_tensor(second_term[:, t0:t1], y[:].indirect(pos2_sb[:, t0 // 16 : t1 // 16]), gates[:, 1, t0:t1], MULT)
-        def warm_up(e, width):
-            idle = psum.tile([P, width], F32, name="idle", tag="bank")
-            second_layer(idle[:], e, slice(0, width))
 
-        if WARM1:
-            warm_up(E - 1, WARM1)
-        for t0, t1 in YS_PARTS:
+        def gated_gather(term, pos_sb, r, t0, t1):
+            listed = pos_sb[:, t0 // PER_COLUMN : t1 // PER_COLUMN]
+            nc.vector.tensor_tensor(term[:, t0:t1], y[:].indirect(listed), gates[:, r, t0:t1], MULT)
+
+        def shared_results(t0, t1):
             ys = psum.tile([P, t1 - t0], F32, name="ys", tag="bank")
             for b in range(t0, t1, P):
                 cols = slice(SLOTS + b, SLOTS + b + P)
@@ -282,24 +263,37 @@ def tile_moe_shr_mlp_relu_kernel(tc, x_words, x_scales, w1, w2, gate, offs, pos1
                     stop=True,
                 )
             nc.scalar.copy(out=shared_turned[:, t0:t1], in_=ys[:])
-        if WARM2:
-            warm_up(SHARED, WARM2)
-        for t0, t1 in V_PARTS:
-            nc.vector.tensor_tensor(result[:, t0:t1], first_turned[:, t0:t1], second_term[:, t0:t1], ADD)
-            nc.sync.dma_start(out=out[:, t0:t1], in_=result[:, t0:t1])
-        def forth(t0, t1):
+
+        def turn_first_term(t0, t1):
             turned = psum.tile([P, t1 - t0], F32, name="turned", tag="bank")
             for b in range(t0, t1, P):
                 nc.tensor.transpose(turned[:, b - t0 : b - t0 + P], first_term[:, b : b + P], identity[:])
             nc.scalar.copy(out=first_turned[:, t0:t1], in_=turned[:])
 
-        def back(t0, t1):
+        def finish(t0, t1):
             partial = psum.tile([P, t1 - t0], F32, name="partial", tag="bank")
-            for i, term in enumerate((shared_turned, first_turned)):
+            for term in (shared_turned, first_turned):
                 for b in range(t0, t1, P):
-                    nc.tensor.matmul(partial[:, b - t0 : b - t0 + P], term[:, b : b + P], identity[:], start=i == 0 and b == t0, stop=i == 1 and b + P == t1, is_transpose=True)
+                    nc.tensor.matmul(
+                        partial[:, b - t0 : b - t0 + P],
+                        term[:, b : b + P],
+                        identity[:],
+                        start=(term is shared_turned and b == t0),
+                        stop=(term is first_turned and b + P == t1),
+                        is_transpose=True,
+                    )
             nc.vector.tensor_tensor(result[:, t0:t1], partial[:], second_term[:, t0:t1], ADD)
             nc.sync.dma_start(out=out[:, t0:t1], in_=result[:, t0:t1])
 
-        for kind, i in SEQ:
-            (forth if kind == 'f' else back)(*PE_PARTS[i])
+        for t0, t1 in PARTS:
+            gated_gather(first_term, pos1_sb, 0, t0, t1)
+        for t0 in (0, T // 2):
+            gated_gather(second_term, pos2_sb, 1, t0, t0 + T // 2)
+        shared_results(0, PART)
+        shared_results(PART, T)
+        turn_first_term(*PARTS[0])
+        finish(*PARTS[0])
+        for part in PARTS[1:]:
+            turn_first_term(*part)
+        for part in PARTS[1:]:
+            finish(*part)

@@ -35,6 +35,9 @@ EXPERTS_A_BANK = 4
 EARLY_W2 = 2
 EARLY_AFTER = 6
 SCALAR_RUN = 3
+RELIEF_FROM = 7
+LATE_COLUMNS = 112
+CLOSING_COLUMNS = 80
 SINGLY_FROM = 6
 PART = 256
 PARTS = [(t0, min(t0 + PART, T)) for t0 in range(0, T, PART)]
@@ -83,14 +86,14 @@ def tile_moe_shr_mlp_relu_kernel(tc, x_words, x_scales, w1, w2, gate, offs, pos1
                 nc.sync.dma_start(out=raw[:, o0:o1, :], in_=w1_rows[e, :, o0:o1, :])
             return raw
 
-        def round_w1(raw, o, on_scalar):
+        def round_w1(raw, o, on_scalar, columns):
             grouped = stage.tile([P, PACK * H], BF16, name="w1_bf16", align_bytes=64)
             src = raw[:, o, :].rearrange("p (j m t) -> p m j t", j=PACK, t=PACK)
             dst = grouped[:].rearrange("p (t m j) -> p m j t", j=PACK, t=PACK)
-            nc.scalar.copy(out=dst[:, :, :, :on_scalar], in_=src[:, :, :, :on_scalar])
+            nc.scalar.copy(out=dst[:, :columns, :, :on_scalar], in_=src[:, :columns, :, :on_scalar])
             nc.vector.tensor_copy(out=dst[:, :, :, HALF:], in_=src[:, :, :, HALF:])
-            if on_scalar < HALF:
-                nc.vector.tensor_copy(out=dst[:, :, :, on_scalar:HALF], in_=src[:, :, :, on_scalar:HALF])
+            if columns < P:
+                nc.vector.tensor_copy(out=dst[:, columns:, :, :on_scalar], in_=src[:, columns:, :, :on_scalar])
             return grouped
 
         def quantize_w1(grouped, tile_runs, pool, name):
@@ -143,7 +146,10 @@ def tile_moe_shr_mlp_relu_kernel(tc, x_words, x_scales, w1, w2, gate, offs, pos1
                     in_=src.rearrange("p (j c i) -> p c j i", i=PACK, j=PACK),
                 )
             else:
-                nc.vector.tensor_copy(out=dst.rearrange("p (n j) -> p n j", j=PACK), in_=src.rearrange("p (j n) -> p n j", j=PACK))
+                nc.vector.tensor_copy(
+                    out=dst.rearrange("p (c i j) -> p c j i", i=PACK, j=PACK),
+                    in_=src.rearrange("p (j c i) -> p c j i", i=PACK, j=PACK),
+                )
 
         def quantize_w2(grouped, e0, e1):
             nc.vector.quantize_mx(
@@ -182,13 +188,11 @@ def tile_moe_shr_mlp_relu_kernel(tc, x_words, x_scales, w1, w2, gate, offs, pos1
             w1_q = []
             for o in range(PASSES):
                 closing = e == LAST and o == PASSES - 1
-                grouped = round_w1(raw, o, 1 if closing else HALF)
+                grouped = round_w1(raw, o, HALF, CLOSING_COLUMNS if closing else LATE_COLUMNS if RELIEF_FROM <= e <= LAST else P)
                 if e == SHARED:
                     w1_q.append(quantize_w1(grouped, [(0, PACK)], keep, "shared%d" % o))
                 else:
-                    if closing:
-                        tile_runs = [(HALF, PACK), (0, 1), (1, HALF)]
-                    elif e == LAST:
+                    if e == LAST:
                         tile_runs = [(HALF, PACK), (0, HALF)]
                     else:
                         tile_runs = [(0, PACK)]
@@ -216,8 +220,9 @@ def tile_moe_shr_mlp_relu_kernel(tc, x_words, x_scales, w1, w2, gate, offs, pos1
         last = stream.tile([P, gate_first + 2 * T], F32, name="last", tag="raw", align_bytes=64)
         w2_raw = last[:, :gate_first].rearrange("p (e w) -> p e w", w=PACK * N)
         gates = last[:, gate_first:].rearrange("p (r t) -> p r t", t=T)
-        for e in range(EARLY_W2, E + 1):
-            nc.sync.dma_start(out=w2_raw[:, e : e + 1, :], in_=w2_rows[:, e : e + 1, :])
+        cuts = list(range(EARLY_W2, SINGLY_FROM, 2)) + list(range(SINGLY_FROM, E + 2))
+        for e0, e1 in zip(cuts, cuts[1:]):
+            nc.sync.dma_start(out=w2_raw[:, e0:e1, :], in_=w2_rows[:, e0:e1, :])
         for r, (pos_sb, pos) in enumerate(((pos1_sb, pos1), (pos2_sb, pos2))):
             nc.sync.dma_start(pos_sb[:], pos)
             nc.sync.dma_start(out=gates[:, r, :], in_=gate[r])

@@ -16,6 +16,7 @@ FP8X4 = mybir.dt.float8_e4m3fn_x4
 MULT = mybir.AluOpType.mult
 ADD = mybir.AluOpType.add
 RELU = mybir.ActivationFunctionType.Relu
+COPY = mybir.ActivationFunctionType.Copy
 
 P = 128
 PACK = 4
@@ -40,14 +41,18 @@ LATE_COLUMNS = 112
 CLOSING_COLUMNS = 80
 SINGLY_FROM = 6
 PART = 256
+TURNED = PART + P
 PARTS = [(t0, min(t0 + PART, T)) for t0 in range(0, T, PART)]
+ROUTED_PASSES = E * PASSES
+CUTS = list(range(0, ROUTED_PASSES - 2, 2)) + list(range(ROUTED_PASSES - 2, ROUTED_PASSES + 1))
+LOADS = list(zip(CUTS, CUTS[1:])) + [(ROUTED_PASSES, ROUTED_PASSES + 2), (ROUTED_PASSES + 2, ROUTED_PASSES + PASSES)]
 
 
 def tile_moe_shr_mlp_relu_kernel(tc, x_words, x_scales, w1, w2, gate, offs, pos1, pos2, out):
     nc = tc.nc
     with ExitStack() as ctx:
         keep = ctx.enter_context(tc.tile_pool(name="keep", bufs=1))
-        stream = ctx.enter_context(tc.tile_pool(name="stream", bufs=4))
+        stream = ctx.enter_context(tc.tile_pool(name="stream", bufs=6))
         stage = ctx.enter_context(tc.tile_pool(name="stage", bufs=2 * PASSES))
         gathered = ctx.enter_context(tc.tile_pool(name="gathered", bufs=SLOTS // GATHER))
         codes = ctx.enter_context(tc.tile_pool(name="codes", bufs=2 * PASSES + 1))
@@ -56,7 +61,7 @@ def tile_moe_shr_mlp_relu_kernel(tc, x_words, x_scales, w1, w2, gate, offs, pos1
         offs_sb = keep.tile([P, SLOTS // PER_COLUMN], U16, name="offs_sb")
         pos1_sb = keep.tile([P, T // PER_COLUMN], U16, name="pos1_sb")
         pos2_sb = keep.tile([P, T // PER_COLUMN], U16, name="pos2_sb")
-        tok_words = keep.tile([P, PASSES, T], I32, name="tok_words", align_bytes=64)
+        tok_words = keep.tile([P, PASSES, T], I32, name="tok_words", align_bytes=256)
         tok_scales = keep.tile([P, T], U8, name="tok_scales", align_bytes=64)
         h_codes = keep.tile([P, SLOTS + T], U32, name="h_codes", align_bytes=64)
         h_scales = keep.tile([P, SLOTS + T], U8, name="h_scales", align_bytes=64)
@@ -64,7 +69,7 @@ def tile_moe_shr_mlp_relu_kernel(tc, x_words, x_scales, w1, w2, gate, offs, pos1
         w2_scales = keep.tile([P, (E + 1) * N], U8, name="w2_scales", align_bytes=64)
         y = keep.tile([P, SLOTS], F32, name="y", align_bytes=64)
 
-        w1_rows = w1.rearrange("e (o p j) c -> e p o (j c)", p=P, j=PACK)
+        w1_rows = w1.rearrange("e (o p j) c -> p (e o) (j c)", p=P, j=PACK)
         w2_rows = w2.rearrange("e (p j) n -> p e (j n)", j=PACK)
 
         def load_token_scales():
@@ -74,21 +79,20 @@ def tile_moe_shr_mlp_relu_kernel(tc, x_words, x_scales, w1, w2, gate, offs, pos1
                 live = slice(QUADRANT * q, QUADRANT * q + SCALE_ROWS * PASSES)
                 nc.gpsimd.dma_start(out=tok_scales[live, :].bitcast(I32), in_=scale_words[:, SCALE_ROWS * q : SCALE_ROWS * (q + 1), :])
 
+        landed = {}
+
         def load_w1(e):
-            if e == LAST:
-                cuts = list(range(PASSES + 1))
-            elif e == LAST - 1:
-                cuts = [0, PASSES - 1, PASSES]
-            else:
-                cuts = [0, PASSES]
-            raw = stream.tile([P, PASSES, PACK * H], F32, name="raw", tag="raw", align_bytes=64)
-            for o0, o1 in zip(cuts, cuts[1:]):
-                nc.sync.dma_start(out=raw[:, o0:o1, :], in_=w1_rows[e, :, o0:o1, :])
-            return raw
+            for g0, g1 in LOADS:
+                if g0 // PASSES == e:
+                    raw = stream.tile([P, g1 - g0, PACK * H], F32, name="raw", tag="raw", align_bytes=256)
+                    nc.sync.dma_start(out=raw[:], in_=w1_rows[:, g0:g1, :])
+                    for g in range(g0, g1):
+                        landed[g] = raw[:, g - g0, :]
+            return [landed[g] for g in range(PASSES * e, PASSES * (e + 1))]
 
         def round_w1(raw, o, on_scalar, columns):
             grouped = stage.tile([P, PACK * H], BF16, name="w1_bf16", align_bytes=64)
-            src = raw[:, o, :].rearrange("p (j m t) -> p m j t", j=PACK, t=PACK)
+            src = raw[o].rearrange("p (j m t) -> p m j t", j=PACK, t=PACK)
             dst = grouped[:].rearrange("p (t m j) -> p m j t", j=PACK, t=PACK)
             nc.scalar.copy(out=dst[:, :columns, :, :on_scalar], in_=src[:, :columns, :, :on_scalar])
             nc.vector.tensor_copy(out=dst[:, :, :, HALF:], in_=src[:, :, :, HALF:])
@@ -208,7 +212,7 @@ def tile_moe_shr_mlp_relu_kernel(tc, x_words, x_scales, w1, w2, gate, offs, pos1
             if e != SHARED:
                 acc = first_layer(w1_q, slot_words, slot_scales, (e * C) % GATHER)
             if e == EARLY_AFTER:
-                early = stream.tile([P, EARLY_W2, PACK * N], F32, name="early", tag="raw", align_bytes=64)
+                early = stream.tile([P, EARLY_W2, PACK * N], F32, name="early", tag="raw", align_bytes=256)
                 nc.sync.dma_start(out=early[:], in_=w2_rows[:, :EARLY_W2, :])
                 early_bf16 = stage.tile([P, EARLY_W2, PACK * N], BF16, name="w2_bf16", bufs=2, align_bytes=64)
                 for i in range(EARLY_W2):
@@ -216,24 +220,31 @@ def tile_moe_shr_mlp_relu_kernel(tc, x_words, x_scales, w1, w2, gate, offs, pos1
                 quantize_w2(early_bf16[:], 0, EARLY_W2)
                 routed_results(0, EARLY_W2)
 
-        gate_first = (E + 1) * PACK * N
-        last = stream.tile([P, gate_first + 2 * T], F32, name="last", tag="raw", align_bytes=64)
-        w2_raw = last[:, :gate_first].rearrange("p (e w) -> p e w", w=PACK * N)
-        gates = last[:, gate_first:].rearrange("p (r t) -> p r t", t=T)
-        cuts = list(range(EARLY_W2, SINGLY_FROM, 2)) + list(range(SINGLY_FROM, E + 2))
+        routed_raw = stream.tile([P, E - EARLY_W2, PACK * N], F32, name="routed_raw", tag="raw", align_bytes=256)
+        gate_first = PACK * N
+        rows_first = gate_first + 2 * T - TURNED
+        last = stream.tile([P, rows_first + P], F32, name="last", tag="raw", align_bytes=256)
+        second_gate = last[:, gate_first : gate_first + T]
+        first_gate = last[:, gate_first + T : rows_first]
+        gate_rows = last[:, rows_first:]
+        nc.vector.memset(gate_rows, 0.0)
+        cuts = list(range(EARLY_W2, SINGLY_FROM, 2)) + list(range(SINGLY_FROM, E + 1))
         for e0, e1 in zip(cuts, cuts[1:]):
-            nc.sync.dma_start(out=w2_raw[:, e0:e1, :], in_=w2_rows[:, e0:e1, :])
-        for r, (pos_sb, pos) in enumerate(((pos1_sb, pos1), (pos2_sb, pos2))):
-            nc.sync.dma_start(pos_sb[:], pos)
-            nc.sync.dma_start(out=gates[:, r, :], in_=gate[r])
+            nc.sync.dma_start(out=routed_raw[:, e0 - EARLY_W2 : e1 - EARLY_W2, :], in_=w2_rows[:, e0:e1, :])
+        nc.sync.dma_start(out=last[:, :gate_first], in_=w2_rows[:, SHARED, :])
+        nc.sync.dma_start(pos1_sb[:], pos1)
+        nc.sync.dma_start(out=first_gate, in_=gate[0, :, TURNED:])
+        nc.sync.dma_start(pos2_sb[:], pos2)
+        nc.sync.dma_start(out=second_gate, in_=gate[1])
+        nc.sync.dma_start(out=gate_rows[: TURNED // P, :], in_=gate[0, 0, :TURNED].rearrange("(b c) -> b c", c=P))
 
         late = stage.tile([P, E + 1 - EARLY_W2, PACK * N], BF16, name="late", bufs=1, align_bytes=64)
         run_end = EARLY_W2 + SCALAR_RUN
         for e in range(EARLY_W2, E + 1):
             if e == run_end:
-                hidden(acc, w2_raw[:, run_end - 1, : PACK * C // 2].bitcast(BF16), LAST * C)
+                hidden(acc, routed_raw[:, SCALAR_RUN - 1, : PACK * C // 2].bitcast(BF16), LAST * C)
             on_scalar = e < run_end or (e != SHARED and (e - run_end) % 2 == 1)
-            round_w2(late[:, e - EARLY_W2, :], w2_raw[:, e, :], on_scalar)
+            round_w2(late[:, e - EARLY_W2, :], last[:, :gate_first] if e == SHARED else routed_raw[:, e - EARLY_W2, :], on_scalar)
         cuts = list(range(EARLY_W2, SINGLY_FROM, 2)) + list(range(SINGLY_FROM, E + 2))
         for e0, e1 in zip(cuts, cuts[1:]):
             quantize_w2(late[:, e0 - EARLY_W2 : e1 - EARLY_W2, :], e0, e1)
@@ -242,19 +253,19 @@ def tile_moe_shr_mlp_relu_kernel(tc, x_words, x_scales, w1, w2, gate, offs, pos1
         for e0, e1 in zip(cuts, cuts[1:]):
             routed_results(e0, e1)
 
-        first_term = keep.tile([P, T], F32, name="first_term")
+        first_raw = keep.tile([P, T], F32, name="first_raw")
         second_term = keep.tile([P, T], F32, name="second_term")
-        result = keep.tile([P, T], F32, name="result")
-        shared_turned = keep.tile([P, T], F32, name="shared_turned")
-        first_turned = keep.tile([P, T], F32, name="first_turned")
+        result = keep.tile([P, T], F32, name="result", align_bytes=256)
+        shared_turned = keep.tile([P, TURNED], F32, name="shared_turned")
+        first_turned = keep.tile([P, TURNED], F32, name="first_turned")
+        gate_cols = keep.tile([P, TURNED // P], F32, name="gate_cols")
         identity = keep.tile([P, P], F32, name="identity")
         make_identity(nc, identity[:])
 
-        def gated_gather(term, pos_sb, r, t0, t1):
-            listed = pos_sb[:, t0 // PER_COLUMN : t1 // PER_COLUMN]
-            nc.vector.tensor_tensor(term[:, t0:t1], y[:].indirect(listed), gates[:, r, t0:t1], MULT)
+        def listed(pos_sb, t0, t1):
+            return y[:].indirect(pos_sb[:, t0 // PER_COLUMN : t1 // PER_COLUMN])
 
-        def shared_results(t0, t1):
+        def shared_turned_part(t0, t1):
             ys = psum.tile([P, t1 - t0], F32, name="ys", tag="bank")
             for b in range(t0, t1, P):
                 cols = slice(SLOTS + b, SLOTS + b + P)
@@ -272,33 +283,40 @@ def tile_moe_shr_mlp_relu_kernel(tc, x_words, x_scales, w1, w2, gate, offs, pos1
         def turn_first_term(t0, t1):
             turned = psum.tile([P, t1 - t0], F32, name="turned", tag="bank")
             for b in range(t0, t1, P):
-                nc.tensor.transpose(turned[:, b - t0 : b - t0 + P], first_term[:, b : b + P], identity[:])
-            nc.scalar.copy(out=first_turned[:, t0:t1], in_=turned[:])
+                nc.tensor.transpose(turned[:, b - t0 : b - t0 + P], first_raw[:, b : b + P], identity[:])
+            for b in range(t0, t1, P):
+                nc.scalar.activation(first_turned[:, b : b + P], turned[:, b - t0 : b - t0 + P], COPY, scale=gate_cols[:, b // P : b // P + 1])
 
-        def finish(t0, t1):
+        def finish(t0, t1, terms):
             partial = psum.tile([P, t1 - t0], F32, name="partial", tag="bank")
-            for term in (shared_turned, first_turned):
+            for term in terms:
                 for b in range(t0, t1, P):
                     nc.tensor.matmul(
                         partial[:, b - t0 : b - t0 + P],
                         term[:, b : b + P],
                         identity[:],
-                        start=(term is shared_turned and b == t0),
+                        start=(term is terms[0] and b == t0),
                         stop=(term is first_turned and b + P == t1),
                         is_transpose=True,
                     )
             nc.vector.tensor_tensor(result[:, t0:t1], partial[:], second_term[:, t0:t1], ADD)
             nc.sync.dma_start(out=out[:, t0:t1], in_=result[:, t0:t1])
 
-        for t0, t1 in PARTS:
-            gated_gather(first_term, pos1_sb, 0, t0, t1)
-        for t0 in (0, T // 2):
-            gated_gather(second_term, pos2_sb, 1, t0, t0 + T // 2)
-        shared_results(0, PART)
-        shared_results(PART, T)
-        turn_first_term(*PARTS[0])
-        finish(*PARTS[0])
-        for part in PARTS[1:]:
-            turn_first_term(*part)
-        for part in PARTS[1:]:
-            finish(*part)
+        gate_turned = psum.tile([P, P], F32, name="gate_turned", tag="bank")
+        nc.tensor.transpose(gate_turned[:], gate_rows, identity[:])
+        for t0, t1 in ((0, PART), (PART, TURNED)):
+            nc.scalar.activation(first_raw[:, t0:t1], listed(pos1_sb, t0, t1), COPY)
+        nc.vector.tensor_tensor(first_raw[:, TURNED:], listed(pos1_sb, TURNED, T), first_gate, MULT)
+        for t0, t1 in ((PART, T), (0, PART)):
+            nc.vector.tensor_tensor(second_term[:, t0:t1], listed(pos2_sb, t0, t1), second_gate[:, t0:t1], MULT)
+        nc.scalar.copy(out=gate_cols[:], in_=gate_turned[:, : TURNED // P])
+        shared_turned_part(0, TURNED)
+        ys_rest = psum.tile([P, T - TURNED], F32, name="ys_rest", tag="bank")
+        second_layer(ys_rest[:], SHARED, slice(SLOTS + TURNED, SLOTS + T))
+        nc.vector.tensor_tensor(first_raw[:, TURNED:], ys_rest[:], first_raw[:, TURNED:], ADD)
+        turn_first_term(0, PART)
+        turn_first_term(PART, TURNED)
+        finish(0, PART, [shared_turned, first_turned])
+        nc.vector.tensor_tensor(result[:, TURNED:], first_raw[:, TURNED:], second_term[:, TURNED:], ADD)
+        nc.sync.dma_start(out=out[:, TURNED:], in_=result[:, TURNED:])
+        finish(PART, TURNED, [shared_turned, first_turned])

@@ -304,7 +304,7 @@ def tile_moe_shr_mlp_relu_kernel(tc, x_words, x_scales, w1, w2, gate, offs, pos1
 
         gate_turned = psum.tile([P, P], F32, name="gate_turned", tag="bank")
         nc.tensor.transpose(gate_turned[:], gate_rows, identity[:])
-        for t0, t1 in ((0, PART), (PART, TURNED)):
+        for t0, t1 in ((0, P), (P, PART), (PART, TURNED)):
             nc.scalar.activation(first_raw[:, t0:t1], listed(pos1_sb, t0, t1), COPY)
         nc.vector.tensor_tensor(first_raw[:, TURNED:], listed(pos1_sb, TURNED, T), first_gate, MULT)
         for t0, t1 in ((PART, T), (0, PART)):
@@ -314,7 +314,8 @@ def tile_moe_shr_mlp_relu_kernel(tc, x_words, x_scales, w1, w2, gate, offs, pos1
         ys_rest = psum.tile([P, T - TURNED], F32, name="ys_rest", tag="bank")
         second_layer(ys_rest[:], SHARED, slice(SLOTS + TURNED, SLOTS + T))
         nc.vector.tensor_tensor(first_raw[:, TURNED:], ys_rest[:], first_raw[:, TURNED:], ADD)
-        turn_first_term(0, PART)
+        turn_first_term(0, P)
+        turn_first_term(P, PART)
         turn_first_term(PART, TURNED)
         finish(0, PART, [shared_turned, first_turned])
         nc.vector.tensor_tensor(result[:, TURNED:], first_raw[:, TURNED:], second_term[:, TURNED:], ADD)

from contextlib import ExitStack

import concourse.mybir as mybir
from concourse.masks import make_identity

K, T, E, C, H, N = 1536, 640, 10, 128, 512, 128
FLOPS = 2 * (E * C + T) * (K * H + H * N)

F32 = mybir.dt.float32
BF16 = mybir.dt.bfloat16
I32 = mybir.dt.int32
U32 = mybir.dt.uint32
U16 = mybir.dt.uint16
U8 = mybir.dt.uint8
FP8X4 = mybir.dt.float8_e4m3fn_x4
MULT = mybir.AluOpType.mult
ADD = mybir.AluOpType.add
RELU = mybir.ActivationFunctionType.Relu
COPY = mybir.ActivationFunctionType.Copy

P = 128
PACK = 4
PASSES = K // (P * PACK)
SLOTS = E * C
SHARED = E
LAST = E - 1
PER_COLUMN = 16
QUADRANT = 32
SCALE_ROWS = 4
TOKEN_BLOCKS = T // C
GATHER = 2 * C
HALF = PACK // 2
TILE_ORDER = (3, 2, 0, 1)
EXPERTS_A_BANK = 4

EARLY_W2 = 2
EARLY_AFTER = 6
SCALAR_RUN = 3
RELIEF_FROM = 7
LATE_COLUMNS = 112
CLOSING_COLUMNS = 80
SINGLY_FROM = 6
PART = 256
TURNED = PART + P
PARTS = [(t0, min(t0 + PART, T)) for t0 in range(0, T, PART)]
ROUTED_PASSES = E * PASSES
CUTS = list(range(0, ROUTED_PASSES - 2, 2)) + list(range(ROUTED_PASSES - 2, ROUTED_PASSES + 1))
LOADS = list(zip(CUTS, CUTS[1:])) + [(ROUTED_PASSES, ROUTED_PASSES + 2), (ROUTED_PASSES + 2, ROUTED_PASSES + PASSES)]


def tile_moe_shr_mlp_relu_kernel(tc, x_words, x_scales, w1, w2, gate, offs, pos1, pos2, out):
    nc = tc.nc
    with ExitStack() as ctx:
        keep = ctx.enter_context(tc.tile_pool(name="keep", bufs=1))
        stream = ctx.enter_context(tc.tile_pool(name="stream", bufs=6))
        stage = ctx.enter_context(tc.tile_pool(name="stage", bufs=2 * PASSES))
        gathered = ctx.enter_context(tc.tile_pool(name="gathered", bufs=SLOTS // GATHER))
        codes = ctx.enter_context(tc.tile_pool(name="codes", bufs=2 * PASSES + 1))
        psum = ctx.enter_context(tc.psum_pool(name="psum", bufs=8))

        offs_sb = keep.tile([P, SLOTS // PER_COLUMN], U16, name="offs_sb")
        pos1_sb = keep.tile([P, T // PER_COLUMN], U16, name="pos1_sb")
        pos2_sb = keep.tile([P, T // PER_COLUMN], U16, name="pos2_sb")
        tok_words = keep.tile([P, PASSES, T], I32, name="tok_words", align_bytes=256)
        tok_scales = keep.tile([P, T], U8, name="tok_scales", align_bytes=64)
        h_codes = keep.tile([P, SLOTS + T], U32, name="h_codes", align_bytes=64)
        h_scales = keep.tile([P, SLOTS + T], U8, name="h_scales", align_bytes=64)
        w2_codes = keep.tile([P, (E + 1) * N], U32, name="w2_codes", align_bytes=64)
        w2_scales = keep.tile([P, (E + 1) * N], U8, name="w2_scales", align_bytes=64)
        y = keep.tile([P, SLOTS], F32, name="y", align_bytes=64)

        w1_rows = w1.rearrange("e (o p j) c -> p (e o) (j c)", p=P, j=PACK)
        w2_rows = w2.rearrange("e (p j) n -> p e (j n)", j=PACK)

        def load_token_scales():
            nc.gpsimd.memset(tok_scales[:], 0)
            scale_words = x_scales.bitcast(I32)
            for q in range(P // QUADRANT):
                live = slice(QUADRANT * q, QUADRANT * q + SCALE_ROWS * PASSES)
                nc.gpsimd.dma_start(out=tok_scales[live, :].bitcast(I32), in_=scale_words[:, SCALE_ROWS * q : SCALE_ROWS * (q + 1), :])

        landed = {}

        def load_w1(e):
            for g0, g1 in LOADS:
                if g0 // PASSES == e:
                    raw = stream.tile([P, g1 - g0, PACK * H], F32, name="raw", tag="raw", align_bytes=256)
                    nc.sync.dma_start(out=raw[:], in_=w1_rows[:, g0:g1, :])
                    for g in range(g0, g1):
                        landed[g] = raw[:, g - g0, :]
            return [landed[g] for g in range(PASSES * e, PASSES * (e + 1))]

        def round_w1(raw, o, on_scalar, columns):
            grouped = stage.tile([P, PACK * H], BF16, name="w1_bf16", align_bytes=64)
            src = raw[o].rearrange("p (j m t) -> p m j t", j=PACK, t=PACK)
            dst = grouped[:].rearrange("p (t m j) -> p m j t", j=PACK, t=PACK)
            nc.scalar.copy(out=dst[:, :columns, :, :on_scalar], in_=src[:, :columns, :, :on_scalar])
            nc.vector.tensor_copy(out=dst[:, :, :, HALF:], in_=src[:, :, :, HALF:])
            if columns < P:
                nc.vector.tensor_copy(out=dst[:, columns:, :, :on_scalar], in_=src[:, columns:, :, :on_scalar])
            return grouped

        def quantize_w1(grouped, tile_runs, pool, name):
            w1_codes = pool.tile([P, H], U32, name=name + "_codes", align_bytes=64)
            w1_scales = pool.tile([P, H], U8, name=name + "_scales", align_bytes=64)
            for tile0, tile1 in tile_runs:
                cols = slice(tile0 * P, tile1 * P)
                nc.vector.quantize_mx(
                    out=w1_codes[:, cols].bitcast(FP8X4),
                    scales=w1_scales[:, cols],
                    in_=grouped[:, PACK * tile0 * P : PACK * tile1 * P],
                )
            return w1_codes, w1_scales

        def gather_slots(first):
            slot_words = gathered.tile([P, PASSES, GATHER], U32, name="slot_words", align_bytes=64)
            slot_scales = gathered.tile([P, GATHER], U8, name="slot_scales", align_bytes=64)
            listed = offs_sb[:, first // PER_COLUMN : (first + GATHER) // PER_COLUMN]
            for o in range(PASSES):
                nc.vector.tensor_copy(slot_words[:, o, :], tok_words[:, o, :].bitcast(U32).indirect(listed))
            nc.vector.tensor_copy(slot_scales[:], tok_scales[:].indirect(listed))
            return slot_words, slot_scales

        def first_layer(w1_q, words, scales, first):
            acc = psum.tile([P, PACK, C], F32, name="acc1", tag="bank")
            cols = slice(first, first + C)
            for o in range(PASSES):
                w1_codes, w1_scales = w1_q[o]
                for t in TILE_ORDER:
                    nc.tensor.matmul_mx(
                        out=acc[:, t, :],
                        lhsT=w1_codes[:, t * P : (t + 1) * P].bitcast(FP8X4),
                        lhsT_scale=w1_scales[:, t * P : (t + 1) * P],
                        rhs=words[:, o, cols].bitcast(FP8X4),
                        rhs_scale=scales[SCALE_ROWS * o :, cols],
                        start=(o == 0 and t == TILE_ORDER[0]),
                        stop=(o == PASSES - 1 and t == TILE_ORDER[-1]),
                    )
            return acc

        def hidden(acc, h, h_first):
            nc.scalar.activation(h.rearrange("p (c t) -> p c t", t=PACK), acc[:].rearrange("p t c -> p c t"), RELU)
            h_cols = slice(h_first, h_first + C)
            nc.vector.quantize_mx(out=h_codes[:, h_cols].bitcast(FP8X4), scales=h_scales[:, h_cols], in_=h)

        def round_w2(dst, src, on_scalar):
            if on_scalar:
                nc.scalar.copy(
                    out=dst.rearrange("p (c i j) -> p c j i", i=PACK, j=PACK),
                    in_=src.rearrange("p (j c i) -> p c j i", i=PACK, j=PACK),
                )
            else:
                nc.vector.tensor_copy(
                    out=dst.rearrange("p (c i j) -> p c j i", i=PACK, j=PACK),
                    in_=src.rearrange("p (j c i) -> p c j i", i=PACK, j=PACK),
                )

        def quantize_w2(grouped, e0, e1):
            nc.vector.quantize_mx(
                out=w2_codes[:, e0 * N : e1 * N].bitcast(FP8X4),
                scales=w2_scales[:, e0 * N : e1 * N],
                in_=grouped.rearrange("p e w -> p (e w)"),
            )

        def second_layer(acc, e, h_cols):
            nc.tensor.matmul_mx(
                out=acc,
                lhsT=w2_codes[:, e * N : (e + 1) * N].bitcast(FP8X4),
                lhsT_scale=w2_scales[:, e * N : (e + 1) * N],
                rhs=h_codes[:, h_cols].bitcast(FP8X4),
                rhs_scale=h_scales[:, h_cols],
                start=True,
                stop=True,
            )

        def routed_results(e0, e1):
            acc = psum.tile([P, e1 - e0, C], F32, name="acc2", tag="bank")
            for e in range(e0, e1):
                second_layer(acc[:, e - e0, :], e, slice(e * C, (e + 1) * C))
            nc.scalar.copy(out=y[:].rearrange("p (e c) -> p e c", c=C)[:, e0:e1, :], in_=acc[:])

        nc.sync.dma_start(out=tok_words[:], in_=x_words.rearrange("o p t r -> p o (t r)").bitcast(I32))
        nc.sync.dma_start(offs_sb[:], offs)

        for step, e in enumerate([SHARED] + list(range(E))):
            raw = load_w1(e)
            if step == 0:
                load_token_scales()
            if e != SHARED and (e * C) % GATHER == 0:
                slot_words, slot_scales = gather_slots(e * C)
            relu_pass = 0 if e in (LAST - 1, LAST) else 1
            w1_q = []
            for o in range(PASSES):
                closing = e == LAST and o == PASSES - 1
                grouped = round_w1(raw, o, HALF, CLOSING_COLUMNS if closing else LATE_COLUMNS if RELIEF_FROM <= e <= LAST else P)
                if e == SHARED:
                    w1_q.append(quantize_w1(grouped, [(0, PACK)], keep, "shared%d" % o))
                else:
                    if e == LAST:
                        tile_runs = [(HALF, PACK), (0, HALF)]
                    else:
                        tile_runs = [(0, PACK)]
                    w1_q.append(quantize_w1(grouped, tile_runs, codes, "w1"))
                if o == 1 and 1 <= step <= TOKEN_BLOCKS:
                    hidden(shared_acc, grouped[:, PACK * C : 2 * PACK * C], SLOTS + (step - 1) * C)
                if o == relu_pass and 1 <= e <= LAST:
                    hidden(acc, grouped[:, : PACK * C], (e - 1) * C)
            if e == SHARED:
                shared_q = w1_q
            if step < TOKEN_BLOCKS:
                shared_acc = first_layer(shared_q, tok_words, tok_scales, step * C)
            if e != SHARED:
                acc = first_layer(w1_q, slot_words, slot_scales, (e * C) % GATHER)
            if e == EARLY_AFTER:
                early = stream.tile([P, EARLY_W2, PACK * N], F32, name="early", tag="raw", align_bytes=256)
                nc.sync.dma_start(out=early[:], in_=w2_rows[:, :EARLY_W2, :])
                early_bf16 = stage.tile([P, EARLY_W2, PACK * N], BF16, name="w2_bf16", bufs=2, align_bytes=64)
                for i in range(EARLY_W2):
                    round_w2(early_bf16[:, i, :], early[:, i, :], i % 2 == 0)
                quantize_w2(early_bf16[:], 0, EARLY_W2)
                routed_results(0, EARLY_W2)

        routed_raw = stream.tile([P, E - EARLY_W2, PACK * N], F32, name="routed_raw", tag="raw", align_bytes=256)
        gate_first = PACK * N
        rows_first = gate_first + 2 * T - TURNED
        last = stream.tile([P, rows_first + P], F32, name="last", tag="raw", align_bytes=256)
        second_gate = last[:, gate_first : gate_first + T]
        first_gate = last[:, gate_first + T : rows_first]
        gate_rows = last[:, rows_first:]
        nc.vector.memset(gate_rows, 0.0)
        cuts = list(range(EARLY_W2, SINGLY_FROM, 2)) + list(range(SINGLY_FROM, E + 1))
        for e0, e1 in zip(cuts, cuts[1:]):
            nc.sync.dma_start(out=routed_raw[:, e0 - EARLY_W2 : e1 - EARLY_W2, :], in_=w2_rows[:, e0:e1, :])
        nc.sync.dma_start(out=last[:, :gate_first], in_=w2_rows[:, SHARED, :])
        nc.sync.dma_start(pos1_sb[:], pos1)
        nc.sync.dma_start(out=first_gate, in_=gate[0, :, TURNED:])
        nc.sync.dma_start(pos2_sb[:], pos2)
        nc.sync.dma_start(out=second_gate, in_=gate[1])
        nc.sync.dma_start(out=gate_rows[: TURNED // P, :], in_=gate[0, 0, :TURNED].rearrange("(b c) -> b c", c=P))

        late = stage.tile([P, E + 1 - EARLY_W2, PACK * N], BF16, name="late", bufs=1, align_bytes=64)
        run_end = EARLY_W2 + SCALAR_RUN
        for e in range(EARLY_W2, E + 1):
            if e == run_end:
                hidden(acc, routed_raw[:, SCALAR_RUN - 1, : PACK * C // 2].bitcast(BF16), LAST * C)
            on_scalar = e < run_end or (e != SHARED and (e - run_end) % 2 == 1)
            round_w2(late[:, e - EARLY_W2, :], last[:, :gate_first] if e == SHARED else routed_raw[:, e - EARLY_W2, :], on_scalar)
        cuts = list(range(EARLY_W2, SINGLY_FROM, 2)) + list(range(SINGLY_FROM, E + 2))
        for e0, e1 in zip(cuts, cuts[1:]):
            quantize_w2(late[:, e0 - EARLY_W2 : e1 - EARLY_W2, :], e0, e1)
        full_banks = E - E % EXPERTS_A_BANK
        cuts = [EARLY_W2] + list(range(EXPERTS_A_BANK, full_banks, EXPERTS_A_BANK)) + list(range(full_banks, E + 1))
        for e0, e1 in zip(cuts, cuts[1:]):
            routed_results(e0, e1)

        first_raw = keep.tile([P, T], F32, name="first_raw")
        second_term = keep.tile([P, T], F32, name="second_term")
        result = keep.tile([P, T], F32, name="result", align_bytes=256)
        shared_turned = keep.tile([P, TURNED], F32, name="shared_turned")
        first_turned = keep.tile([P, TURNED], F32, name="first_turned")
        gate_cols = keep.tile([P, TURNED // P], F32, name="gate_cols")
        identity = keep.tile([P, P], F32, name="identity")
        make_identity(nc, identity[:])

        def listed(pos_sb, t0, t1):
            return y[:].indirect(pos_sb[:, t0 // PER_COLUMN : t1 // PER_COLUMN])

        def shared_turned_part(t0, t1):
            ys = psum.tile([P, t1 - t0], F32, name="ys", tag="bank")
            for b in range(t0, t1, P):
                cols = slice(SLOTS + b, SLOTS + b + P)
                nc.tensor.matmul_mx(
                    out=ys[:, b - t0 : b - t0 + P],
                    lhsT=h_codes[:, cols].bitcast(FP8X4),
                    lhsT_scale=h_scales[:, cols],
                    rhs=w2_codes[:, SHARED * N :].bitcast(FP8X4),
                    rhs_scale=w2_scales[:, SHARED * N :],
                    start=True,
                    stop=True,
                )
            nc.scalar.copy(out=shared_turned[:, t0:t1], in_=ys[:])

        def turn_first_term(t0, t1):
            turned = psum.tile([P, t1 - t0], F32, name="turned", tag="bank")
            for b in range(t0, t1, P):
                nc.tensor.transpose(turned[:, b - t0 : b - t0 + P], first_raw[:, b : b + P], identity[:])
            for b in range(t0, t1, P):
                nc.scalar.activation(first_turned[:, b : b + P], turned[:, b - t0 : b - t0 + P], COPY, scale=gate_cols[:, b // P : b // P + 1])

        def finish(t0, t1, terms):
            partial = psum.tile([P, t1 - t0], F32, name="partial", tag="bank")
            for term in terms:
                for b in range(t0, t1, P):
                    nc.tensor.matmul(
                        partial[:, b - t0 : b - t0 + P],
                        term[:, b : b + P],
                        identity[:],
                        start=(term is terms[0] and b == t0),
                        stop=(term is first_turned and b + P == t1),
                        is_transpose=True,
                    )
            nc.vector.tensor_tensor(result[:, t0:t1], partial[:], second_term[:, t0:t1], ADD)
            nc.sync.dma_start(out=out[:, t0:t1], in_=result[:, t0:t1])

        gate_turned = psum.tile([P, P], F32, name="gate_turned", tag="bank")
        nc.tensor.transpose(gate_turned[:], gate_rows, identity[:])
        for t0, t1 in ((0, P), (P, PART), (PART, TURNED)):
            nc.scalar.activation(first_raw[:, t0:t1], listed(pos1_sb, t0, t1), COPY)
        nc.vector.tensor_tensor(first_raw[:, TURNED:], listed(pos1_sb, TURNED, T), first_gate, MULT)
        for t0, t1 in ((PART, T), (0, PART)):
            nc.vector.tensor_tensor(second_term[:, t0:t1], listed(pos2_sb, t0, t1), second_gate[:, t0:t1], MULT)
        nc.scalar.copy(out=gate_cols[:], in_=gate_turned[:, : TURNED // P])
        shared_turned_part(0, TURNED)
        ys_rest = psum.tile([P, T - TURNED], F32, name="ys_rest", tag="bank")
        second_layer(ys_rest[:], SHARED, slice(SLOTS + TURNED, SLOTS + T))
        nc.vector.tensor_tensor(first_raw[:, TURNED:], ys_rest[:], first_raw[:, TURNED:], ADD)
        turn_first_term(0, P)
        turn_first_term(P, PART)
        turn_first_term(PART, TURNED)
        finish(0, PART, [shared_turned, first_turned])
        nc.vector.tensor_tensor(result[:, TURNED:], first_raw[:, TURNED:], second_term[:, TURNED:], ADD)
        nc.sync.dma_start(out=out[:, TURNED:], in_=result[:, TURNED:])
        finish(PART, TURNED, [shared_turned, first_turned])
